import numpy as np, ml_dtypes
CORES = [2,6,10,14,18,22,26,30]
N = 8
BF = ml_dtypes.bfloat16
M, L, KH, CAP, RO, OC = 4096, 256, 10, 32, 3, 4096
S = 16
def pack(b, o, w):
    return {"ball": np.ascontiguousarray(b.reshape(N, 128, M)).astype(np.float32).astype(BF), "stk": np.ascontiguousarray(o.reshape(N, 128, L)).astype(np.int32),
            "wt": np.ascontiguousarray(w.reshape(N, 128, 1)).astype(np.float32).astype(BF)}
def halves(rng):
    bright = np.argsort(rng.random((N, 8, M)), axis=-1) < M // 2
    return np.where(bright[:, :, None], rng.integers(140, 256, (N, 8, 16, M)), rng.integers(0, 120, (N, 8, 16, M))), bright
def stacks(rng, kk, bright):
    br, di = np.flatnonzero(bright), np.flatnonzero(~bright); dep = np.arange(16)[:, None]
    o = rng.integers(0, M, (16, L)); top = np.where(kk > 0, rng.choice(br, L), rng.choice(di, L))
    o = np.where((dep > 0) & (dep <= kk), rng.choice(di, (16, L)), o)
    o = np.where(dep == kk + 1, np.where(kk > 0, top, rng.choice(br, L)), o)
    o[0] = top
    return o
def later(rng, z):
    kk = np.concatenate([np.full(L // 2, 15), np.zeros(z, np.int64), rng.integers(1, KH, L - L // 2 - z)])
    kk[:int(np.sum(kk)) % S] = 14
    kk = rng.permutation(kk); dep = np.arange(16)[:, None]
    kind = rng.permutation(np.arange(M - L) % 3)
    b = rng.integers(0, 256, (16, M))
    b[:, L:] = np.where(kind == 0, rng.integers(0, 40, (16, M - L)), np.where(kind == 1, rng.integers(60, 200, (16, M - L)), 255))
    low, mid, top = L + np.flatnonzero(kind == 0), L + np.flatnonzero(kind == 1), L + np.flatnonzero(kind == 2)
    o = np.where((dep > 0) & (dep <= kk), rng.choice(mid, (16, L)), rng.integers(0, M, (16, L)))
    o = np.where(dep == kk + 1, rng.choice(top, (16, L)), o)
    o[0] = rng.choice(low, L)
    return b, o
def quiet(rng, a):
    c = np.arange(M) // L; free = rng.permutation(np.flatnonzero((c > 0) & (c != a)))
    low, top = free[:16], free[16:M // 2]
    b = rng.integers(0, 256, (16, M)); b[:, low] = 0; b[:, top] = 255
    o = rng.integers(0, M, (16, L)); one = rng.permutation(L) < a
    o[0] = np.where(one, rng.choice(top, L), o[0]); o[1] = np.where(one, rng.choice(low, L), rng.choice(top, L)); o[2] = np.where(one, rng.choice(top, L), o[2])
    return b, o
def setup_inputs(rng):
    lev = rng.integers(0, 256, (N, 8, 1, M))
    b = np.clip(lev + np.rint(24 * rng.standard_normal((N, 8, 16, M), dtype=np.float32)).astype(np.int64), 0, 255)
    o = rng.integers(0, M, (N, 8, 16, L)); high = np.argsort(lev[:, :, 0], axis=-1)[..., M - M // 8:]
    pick = np.take_along_axis(high, rng.integers(0, M // 8, (N, 8, L)), 2); share = rng.choice(np.array([0.0, 0.1, 0.3, 0.5]), (N, 8, 1))
    o[:, :, 0] = np.where(rng.random((N, 8, L)) < share, pick, o[:, :, 0])
    return pack(b, o, rng.integers(0, 256, (N, 8, 16, 1)))
def setup_inputs_room(rng):
    b, bright = halves(rng); o = np.zeros((N, 8, 16, L), np.int64); c = np.array([0, 1, CAP - 1, CAP, CAP + 1, L])
    for q in range(N):
        for g in range(8):
            n, z = int(rng.choice(c)), int(rng.choice(c))
            if q in (0, 2): n = (CAP, CAP + 1, L, CAP - 1, 1, 0, CAP, CAP + 1)[g]
            if q in (1, 3):
                z = (CAP, CAP + 1, CAP, CAP, 0, L, CAP - 1, 1)[g]; n = min(n, L - z)
            z = min(z, L - n)
            kk = np.concatenate([rng.choice(np.array([KH, KH, KH + 1, 15]), n), np.zeros(z, np.int64), rng.choice(np.array([1, KH // 2, KH - 1, KH - 1]), L - n - z)])
            kk = rng.permutation(kk)
            if q in (0, 2) and g == 0:
                i = int(np.flatnonzero(kk >= KH)[0]); kk[[i, L - 1]] = kk[[L - 1, i]]
            if q in (1, 3) and g < 3: kk = kk[np.argsort(kk > 0, kind="stable")]
            o[q, g] = stacks(rng, kk, bright[q, g])
    return pack(b, o, rng.integers(0, 256, (N, 8, 16, 1)))
def setup_inputs_votes(rng):
    base = rng.integers(1, 255, (N, 8, 16, 1)); j = rng.choice(np.array([7, 8, 9, 10, 16]), (N, 8, 1, M), p=[0.04, 0.06, 0.5, 0.2, 0.2])
    place = np.argsort(rng.random((N, 8, 16, M)), axis=2)
    b = base - (place < j) + (place >= j) * rng.integers(0, 2, (N, 8, 16, M))
    b[..., ::4] = base
    o = 4 * rng.integers(0, M // 4, (N, 8, 16, L)) + rng.integers(1, 4, (N, 8, 16, L))
    o[:, :, 0] = np.where(rng.random((N, 8, L)) < 0.7, 4 * rng.integers(0, M // 4, (N, 8, L)), o[:, :, 0])
    return pack(b, o, rng.integers(0, 256, (N, 8, 16, 1)))
def setup_inputs_ends(rng):
    b, bright = halves(rng); b[..., 0] = 255; b[..., M - 1] = 0; bright[..., 0] = True; bright[..., M - 1] = False
    b[:, 4, :, 1023] = 255; b[:, 4, :, M - 16] = 0; bright[:, 4, 1023] = True; bright[:, 4, M - 16] = False
    o = np.zeros((N, 8, 16, L), np.int64); w = rng.integers(0, 256, (N, 8, 16, 1)); w[:, 0::2] = 255; w[:, 1] = 0; w[:, 5:] = 0
    for q in range(N):
        for g in range(8):
            kk = rng.integers(0, 16, L); kk[0] = 15 * (q % 2); kk[L - 1] = 15 * (1 - q % 2)
            if g == 4: kk[:] = 15
            if g == 6: b[q, g], o[q, g] = quiet(rng, int(rng.integers(1, S)))
            elif g in (5, 7): b[q, g], o[q, g] = later(rng, (0, 1, CAP // 2, CAP - 1)[(q + g) % 4])
            else: o[q, g] = stacks(rng, kk, bright[q, g])
    o[:, 0] = rng.choice(np.array([M - 1, M - 1, M - 1, M - 1, M - 1, M - 1, 0]), (N, 16, L))
    o[:, 0, 0] = rng.choice(np.array([0, 0, M - 1]), (N, L))
    o[:, 2] = o[:, 2, :1]
    far = np.where(np.arange(16)[:, None] == 0, 1023, rng.choice(np.array([M - 1, M - 16]), (N, 16, L)))
    o[:, 4] = np.where(rng.random((N, 1, L)) < 0.25, far, o[:, 4])
    return pack(b, o, w)
def setup_inputs_spread(rng):
    b = np.minimum(np.exp2(8.5 * rng.random((N, 8, 1, M))) * rng.random((N, 8, 16, M)), 255.0).astype(np.int64) * (rng.random((N, 8, 1, M)) > 0.0625)
    w = np.exp2(8 * rng.random((N, 8, 16, 1))).astype(np.int64) - 1
    o = (M * rng.random((N, 8, 16, L)) ** rng.choice(np.array([1, 2, 4]), (N, 8, 1, 1))).astype(np.int64)
    return pack(b, o, w)
def check_inputs(d):
    bad = []
    for k, hi in (("ball", 255), ("stk", M - 1), ("wt", 255)):
        v = np.asarray(d[k]).astype(np.float64)
        if not (np.min(v) >= 0 and np.max(v) <= hi): bad.append("range of " + k)
        elif np.any(v != np.floor(v)): bad.append("whole numbers in " + k)
    return bad
def reference(ball, stk, wt):
    b = ball.astype(np.float32).astype(np.int64).reshape(N, 8, 16, M)
    o = stk.astype(np.int64).reshape(N, 8, 16, L)
    w = wt.astype(np.float32).astype(np.int64).reshape(N, 8, 16, 1)
    lane = np.arange(L); dep = np.arange(16)[:, None]
    for t in range(RO):
        p = np.take_along_axis(b, o.reshape(N, 8, 1, 16 * L), 3).reshape(N, 8, 16, 16, L)
        x, rest = p[:, :, :, 0], p[:, :, :, 1:]
        won = np.add.reduce((x[:, :, :, None] > rest).astype(np.int64), axis=2) >= 9
        crossed = np.multiply.accumulate(won.astype(np.int64), axis=2)
        k = np.add.reduce(crossed, axis=2)
        top = np.where(k[:, :, None] == 0, 255, np.max(rest * crossed[:, :, None], axis=3))
        y = np.abs(x - top)
        A = np.add.reduce(k, axis=2)
        v = L * ((np.add.reduce(w * y, axis=2) + A[:, :, None]) & (S - 1)) + lane
        new = (((o * (2 * (o[:, :, :1] & 1023) + 1)) >> 4) + A[:, :, None, None]) & (M - 1)
        up = np.concatenate([new[:, :, 1:], new[:, :, :1]], axis=2)
        o = np.where(dep < k[:, :, None], up, np.where(dep == k[:, :, None], v[:, :, None], o))
        z = y.copy()
        for r in range(N):
            q = (r - 1 - t) % N
            for g in range(8):
                src = np.flatnonzero(k[q, g] >= KH)[:CAP]; dst = np.flatnonzero(k[r, g] == 0)[:len(src)]
                z[r, g][:, dst] = y[q, g][:, src[:len(dst)]]
        np.put_along_axis(b, v[:, :, None, :], z, 3)
    return {"yo": o.reshape(N, 128, L).astype(np.float32), "yb": b.reshape(N, 128, M)[:, :, :OC].astype(np.float32).astype(BF)}

@@ -1,0 +1,394 @@
+import numpy as np
+from concourse.mybir import AluOpType, AxisListType, ActivationFunctionType
+
+OP = AluOpType
+AF = ActivationFunctionType
+ROUNDS = 3
+NB = 4096
+DUMP = 32
+CH = 4
+CW = NB // CH
+REP = 4
+
+SCRATCH = {}
+
+
+def _declare(where, dtype, **shapes):
+    for name, n in shapes.items():
+        SCRATCH[name] = (where, [128] + (n if isinstance(n, list) else [n]), dtype)
+
+
+_declare("sbuf", "bfloat16", B=NB + DUMP, P=NB, PM=NB, pat=64, WN=[16, 256], tw=256, st=256, K=256, D=256, Y=272, HF=256,
+         ZF=256, CH=256, CZ=256, J0=256, J1=256, C=256, EK=256, ob=256, o256=256, r57=256, ID=128, B1=128, BO=128, BA=128,
+         WB=128, E1=144, E2=144, E01=144, WE=144, RS=CW, KS=256, KT=16, HT=16, ET=16, iL=16, row=256, wb=1, OW=32, u=32,
+         w=32, PK0=32, PK1=32, PK2=32, RX0=32, RX1=32, RX2=32)
+_declare("sbuf", "float32", S16=256, kb=16, krr=1, acca=2, accb=2, accp=2, accz=2, vraw=272, G32=32, GM=32, rd=2, nk=2,
+         nd=2, ef=256, zu=256, t3=256, yof=256, of32=128, c16=128, cm1=128, LE=128, LS=128, NI=128, rc=1, d16=1, bs=2,
+         nc=2, dm=2, j16=16, iF=16, KB=16, rowf=256, cm=32, DM=32, wf=1)
+_declare("sbuf", "int32", SI=256, eI=256, UI=256, VI=16, VB=16, ri=2, rb=2, pI=1, rI=1, wI=1, wA=1)
+_declare("sbuf", "uint16", SU=256, kl0=16, kl1=16, hl=2, zl=2, OL=2, VL=16)
+_declare("psum", "float32", psX0=512, psX1=512, psV=512, psE=512, psD=512, psS=512, psR=512, psL=512)
+
+DMAS = ["in_stk", "in_wt", "in_ball", "out_yo", "out_yb"]
+SEMAPHORES = ["qv", "qs", "qt", "qg", "ls"] + ["dma_" + d for d in DMAS] + ["arr%d" % t for t in range(ROUNDS)]
+
+
+def rank_program(g, core, T, topo):
+    rank = T.rank_of(core)
+    if rank is None:
+        return
+    queues = {"g": g, "v": g.vector, "s": g.scalar, "t": g.tensor, "y": g.sync}
+    qsem = {"g": "qg", "v": "qv", "s": "qs", "t": "qt"}
+    total = {}
+    know = dict((q, {}) for q in queues)
+    hist = {}
+
+    def wait_for(q, sem, val, clock):
+        if know[q].get(sem, 0) >= val:
+            return
+        queues[q].wait_ge(T.sem[sem], val)
+        know[q][sem] = val
+        for s2, v2 in clock.items():
+            if know[q].get(s2, 0) < v2:
+                know[q][s2] = v2
+
+    def need(q, reads, writes, waw=True):
+        deps = []
+        for acc, isw in ((reads, False), (writes, True)):
+            for (b, lo, hi) in acc:
+                for h in hist.get(b, ()):
+                    same = h[3] == q
+                    if b.startswith("ps") and not same:
+                        deps.append(h)
+                        continue
+                    if h[1] <= lo or hi <= h[0] or not (isw or h[2]):
+                        continue
+                    if same and (q == "t" or (isw and (not h[2] or not waw))):
+                        continue
+                    deps.append(h)
+        for h in sorted(deps, key=lambda h: -h[5]):
+            wait_for(q, h[4], h[5], h[6])
+
+    def note(q, sem, val, reads, writes):
+        clock = dict(know.get(q, {}))
+        clock[sem] = max(clock.get(sem, 0), val)
+        for acc, isw in ((reads, False), (writes, True)):
+            for (b, lo, hi) in acc:
+                old = hist.get(b, [])
+                if isw and b.startswith("ps"):
+                    old = []
+                elif isw:
+                    old = [h for h in old if not (lo <= h[0] and h[1] <= hi)]
+                else:
+                    old = [h for h in old if not (h[3] == q and not h[2] and lo <= h[0] and h[1] <= hi)]
+                hist[b] = old + [(lo, hi, isw, q, sem, val, clock)]
+
+    def reg(r):
+        return r if isinstance(r, tuple) else (r, 0, int(np.prod(SCRATCH[r][1][1:])))
+
+    def do(q, call, reads, writes, waw=True):
+        R, W = [reg(r) for r in reads], [reg(w) for w in writes]
+        need(q, R, W, waw)
+        sem = qsem[q]
+        total[sem] = total.get(sem, 0) + 1
+        call(queues[q]).then_inc(T.sem[sem], 1)
+        note(q, sem, total[sem], R, W)
+
+    def dma(q, name, out, in_, reads, writes):
+        R, W = [reg(r) for r in reads], [reg(w) for w in writes]
+        need(q, R, W)
+        sem = "dma_" + name
+        total[sem] = 16
+        queues[q].dma_start(out, in_).then_inc(T.sem[sem], 16)
+        note(sem, sem, 16, R, W)
+
+    def lanes_of(src, dst):
+        return topo.engines(src, dst)[:8]
+
+    def send(dst, src, out, reads, sem):
+        need("g", [reg(r) for r in reads], [])
+        rid, pid, _ = topo.addr(dst)
+        eng = lanes_of(core, dst)
+        total["ls"] = total.get("ls", 0) + len(eng)
+        g.remote_dma(out, src, T.sem[sem], T.sem["ls"], pid, rid, sum(1 << e for e in eng))
+
+    def landed(frm, sem, name):
+        total[sem] = len(lanes_of(frm, core))
+        note("remote", sem, total[sem], [], [reg(name)])
+
+    def ts(out, in0, s1, s2, op0, op1, R, W):
+        ops = (op0,) if op1 is None else (op0, op1)
+        do("v", lambda v: v.tensor_scalar(out, in0, s1, s2, *ops), R, W)
+
+    def tt(out, a, b, op, R, W, waw=True):
+        do("v", lambda v: v.tensor_tensor(out, a, b, op), R, W, waw)
+
+    def cp(out, a, R, W):
+        do("v", lambda v: v.tensor_copy(out, a), R, W)
+
+    def ms(out, c, W):
+        do("v", lambda v: v.memset(out, c), [], W)
+
+    def scan(out, d0, d1, o0, o1, R, W, ini=0.0):
+        do("v", lambda v: v.tensor_tensor_scan(out, d0, d1, ini, o0, o1), R, W)
+
+    def act(out, a, f, R, W, **kw):
+        do("s", lambda s: s.activation(out, a, f, **kw), R, W)
+
+    def mm(out, l, r, start, stop, R, W):
+        do("t", lambda x: x.matmul(out, l, r, start, stop), R, W)
+
+    def asel(out, a, pat, cmp, fill, base, mult, R, W):
+        do("g", lambda x: x.affine_select(out, a, pat, cmp, fill, base, mult), R, W)
+
+    def iota(out, pat, base, mult, W, **kw):
+        do("g", lambda x: x.iota(out, pat, base, mult, **kw), [], W)
+
+    small = {"allow_small_or_imprecise_dtypes": True}
+
+    dma("y", "in_stk", T.SI[:], T.stk[:], [], ["SI"])
+    dma("s", "in_ball", T.B[:, 0:NB], T.ball[:], [], [("B", 0, NB)])
+    dma("y", "in_wt", T.wb[:], T.wt[:], [], ["wb"])
+
+    iota(T.pI[:], [[0, 1]], 0, 1, ["pI"])
+    ms(T.of32[:], 1.0, ["of32"])
+    ms(T.cm1[:], -1.0, ["cm1"])
+    ms(T.ob[:], 1.0, ["ob"])
+    ms(T.c16[:], 0.0625, ["c16"])
+    blk = [[-16, 8], [0, 16]]
+    asel(T.LE[:], T.of32[:], blk, OP.is_equal, 0.0, 0, 1, ["of32"], ["LE"])
+    asel(T.ID[:], T.ob[:, 0:128], [[-1, 128]], OP.is_equal, 0.0, 0, 1, ["ob"], ["ID"])
+    asel(T.NI[:], T.cm1[:], [[-1, 128]], OP.is_equal, 0.0, 0, 1, ["cm1"], ["NI"])
+    iota(T.rowf[:], [[16, 256]], 0, 0, ["rowf"], **small)
+    iota(T.j16[:], [[16, 16]], 0, 0, ["j16"], **small)
+    iota(T.cm[:], [[0, 2], [1, 16]], 0, 0, ["cm"], **small)
+    iota(T.KT[:], [[16, 16]], 0, 0, ["KT"], **small)
+    asel(T.E1[:], T.ob[:, 0:144], [[-16, 9], [0, 16]], OP.is_ge, 0.0, 0, 1, ["ob"], ["E1"])
+    asel(T.E2[:], T.E1[:], [[16, 9], [0, 16]], OP.is_ge, 0.0, 15, -1, ["E1"], ["E2"])
+    asel(T.E01[:], T.E2[:], [[0, 9], [1, 16]], OP.is_equal, 0.0, -15, 0, ["E2"], ["E01"])
+    asel(T.LS[:], T.c16[:], [[-1, 128]], OP.is_equal, 0.0, -1, 1, ["c16"], ["LS"])
+    asel(T.B1[:], T.ob[:, 0:128], blk, OP.is_ge, 0.0, 0, 1, ["ob"], ["B1"])
+    asel(T.BO[:], T.B1[:], [[16, 8], [0, 16]], OP.is_ge, 0.0, 15, -1, ["B1"], ["BO"])
+
+    ms(T.pat[:], 0.0, ["pat"])
+    ms(T.RS[:], 1.0, ["RS"])
+    ms(T.r57[:], 57344.0, ["r57"])
+    ms(T.RS[:, 1:CW:16], 0.0, ["RS"])
+    ms(T.KS[:], -1.0, ["KS"])
+    ms(T.pat[:, 0:64:16], 16.0, ["pat"])
+    ms(T.o256[:], 256.0, ["o256"])
+    ms(T.KS[:, 0:256:16], 100.0, ["KS"])
+    ms(T.B[:, NB:NB + DUMP], 0.0, [("B", NB, NB + DUMP)])
+    ms(T.Y[:, 256:272], -512.0, [("Y", 256, 272)])
+    ms(T.vraw[:, 256:272], 0.0, [("vraw", 256, 272)])
+    cp(T.SU[:], T.SI[:], ["SI"], ["SU"])
+
+    def early_constants():
+        ts(T.rI[:], T.pI[:], 15, None, OP.bitwise_and, None, ["pI"], ["rI"])
+        cp(T.row[:], T.rowf[:], ["rowf"], ["row"])
+        cp(T.rc[:], T.rI[:], ["rI"], ["rc"])
+        ts(T.HT[:], T.KT[:], 160.0, None, OP.is_ge, None, ["KT"], ["HT"])
+        ts(T.iF[:], T.j16[:], T.rc[:], None, OP.add, None, ["j16", "rc"], ["iF"])
+        ts(T.d16[:], T.rc[:], 16.0, None, OP.mult, None, ["rc"], ["d16"])
+        ts(T.nc[:, 0:1], T.rc[:], 0.0, None, OP.add, None, ["rc"], [("nc", 0, 1)])
+        ts(T.nc[:, 1:2], T.rc[:], 16.0, None, OP.add, None, ["rc"], [("nc", 1, 2)])
+        ts(T.KB[:], T.iF[:], 16.0, 14.0, OP.mult, OP.add, ["iF"], ["KB"])
+        ts(T.ET[:], T.KT[:], T.d16[:], None, OP.is_equal, None, ["KT", "d16"], ["ET"])
+        ts(T.iL[:], T.iF[:], 16.0, None, OP.mult, None, ["iF"], ["iL"])
+        ts(T.DM[:], T.cm[:], T.rc[:], None, OP.is_equal, None, ["cm", "rc"], ["DM"])
+        ts(T.bs[:], T.nc[:], -1.0, -0.5, OP.mult, OP.add, ["nc"], ["bs"])
+        ts(T.dm[:], T.nc[:], float(NB), None, OP.add, None, ["nc"], ["dm"])
+        cp(T.wI[:], T.wb[:], ["wb"], ["wI"])
+        ts(T.wA[:], T.wI[:], 15, None, OP.bitwise_and, None, ["wI"], ["wA"])
+        ts(T.wf[:], T.wA[:], 4096.0, None, OP.mult, None, ["wA"], ["wf"])
+
+    def late_constants():
+        ts(T.WE[:], T.E01[:], T.wf[:], None, OP.mult, None, ["E01", "wf"], ["WE"])
+        ts(T.WB[:], T.BO[:], T.wf[:], None, OP.mult, None, ["BO", "wf"], ["WB"])
+
+    balls, spare = T.B[:, 0:NB], T.B[:, 0:NB + DUMP]
+    ones, row = T.ob[0:1, 0:128], T.row[0:1, :]
+    psD, psS, psR, psL = T.psD[:, 0:256], T.psS[:, 0:256], T.psR[:, 0:256], T.psL[:, 0:16]
+
+    def factors():
+        ts(T.eI[:], T.SI[:], 1023, None, OP.bitwise_and, None, ["SI"], ["eI"])
+        ts(T.S16[:], T.SI[:], 16.0, None, OP.mult, None, ["SI"], ["S16"])
+        ts(T.ef[:], T.eI[:], 2.0, 1.0, OP.mult, OP.add, ["eI"], ["ef"])
+        mm(T.psE[:, 0:256], T.LE[:], T.ef[:], True, True, ["LE", "ef"], ["psE"])
+
+    factors()
+    early_constants()
+
+    for t in range(ROUNDS):
+        last = t == ROUNDS - 1
+        n = len(T.cores)
+        dst, frm = T.cores[(rank + t + 1) % n], T.cores[(rank - t - 1) % n]
+        PKn, RXn = "PK%d" % t, "RX%d" % t
+
+        def part(name, c):
+            return (name, CW * c, CW * c + CW)
+
+        def gather(q, a, b):
+            out, off = T.P[:, 16 * a:16 * b], T.SU[:, a:b]
+            R, W = [("B", 0, NB), ("SU", a, b)], [("P", 16 * a, 16 * b)]
+            if q == "s":
+                act(out, balls.indirect(off), AF.Copy, R, W)
+            else:
+                cp(out, balls.indirect(off), R, W)
+
+        def tops(c):
+            b = "psX%d" % (c % 2)
+            for r in range(REP):
+                mm(T[b][:, r:64 * REP:REP], T.ID[:], T.P[:, CW * c:CW * c + CW:16], True, True, ["ID", part("P", c)], [b])
+
+        def compare(c):
+            b, s = "psX%d" % (c % 2), 16 // REP
+            for d in range(s):
+                tt(T.WN[:, 4 * c:4 * c + 4, d:256:s], T.P[:, CW * c + d:CW * c + CW:s], T[b][:, 0:64 * REP],
+                   OP.is_lt, [part("P", c), b], [part("WN", c)], waw=False)
+
+        def votes(c, b):
+            mm(T[b][:, 64 * c:64 * c + 64], ones, T.pat[0:1, :], True, False, ["ob", "pat"], [b])
+            for q in range(16):
+                mm(T[b][:, 64 * c:64 * c + 64], T.E01[:, 15 - q:143 - q], T.WN[:, 4 * c:4 * c + 4, 16 * q:16 * q + 16],
+                   False, q == 15, ["E01", part("WN", c)], [b])
+
+        def prefix(c):
+            scan(T.PM[:, CW * c:CW * c + CW], T.RS[:], T.P[:, CW * c:CW * c + CW], OP.mult, OP.max,
+                 ["RS", part("P", c)], [part("PM", c)])
+
+        def filled(c, e):
+            a, e = CW * c, CW * e
+            act(T.PM[:, a:e:16], T.P[:, a:e:16], AF.Identity, [("P", a, e)], [("PM", a, e)], bias=255.0, scale=0.0)
+
+        def won(a, e, b):
+            ts(T.tw[:, a:e], T[b][:, a:e], 9.0, 16.0, OP.is_ge, OP.mult, [b], [("tw", a, e)])
+
+        def runs(a, e):
+            scan(T.st[:, a:e], T.KS[:, a:e], T.tw[:, a:e], OP.add, OP.min, ["KS", ("tw", a, e)], [("st", a, e)])
+
+        def klist(j, e):
+            ts(T.kl0[:, j:e], T.st[:, 16 * j + 15:16 * e:16], 14.0, None, OP.add, None, [("st", 16 * j, 16 * e)], [("kl0", j, e)])
+
+        def high(j, e):
+            act(T.HF[:, 16 * j:16 * e], T.HT[:, 0:16].indirect(T.kl0[:, j:e]), AF.Copy, ["HT", ("kl0", j, e)], [("HF", 16 * j, 16 * e)])
+
+        def count(a, e, acc):
+            for c in range(2):
+                act(T["J%d" % c][:, a:e], T.CH[:, a:e], AF.Sign, [("CH", a, e), "bs"], ["J%d" % c, (acc, c, c + 1)],
+                    bias=T.bs[:, c:c + 1], accum_out=T[acc][:, c:c + 1])
+
+        gather("s", 0, 32)
+        gather("v", 32, 64)
+        gather("s", 64, 128)
+        gather("s", 128, 192)
+        gather("s", 192, 256)
+        tops(0)
+        compare(0)
+        mm(psD, T.NI[:], T.S16[:], True, False, ["NI", "S16"], ["psD"])
+        mm(psD, ones, T.r57[0:1, :], False, False, ["ob", "r57"], ["psD"])
+        mm(psR, ones, row, True, False, ["ob", "row"], ["psR"])
+        mm(psL, T.ID[:], T.iL[:], True, False, ["ID", "iL"], ["psL"])
+        tops(1)
+        votes(0, "psV")
+        tt(T.zu[:], T.S16[:], T.psE[:, 0:256], OP.mult, ["S16", "psE"], ["zu"])
+        tops(2)
+        prefix(0)
+        compare(1)
+        votes(1, "psV")
+        mm(psD, T.LS[:], T.zu[:], False, False, ["LS", "zu"], ["psD"])
+        if t == 0:
+            late_constants()
+        tops(3)
+        prefix(1)
+        compare(2)
+        votes(2, "psV")
+        prefix(2)
+        filled(0, 3)
+        compare(3)
+        votes(3, "psE")
+        mm(psS, T.NI[:], T.S16[:], True, False, ["NI", "S16"], ["psS"])
+        mm(psS, ones, row, False, False, ["ob", "row"], ["psS"])
+
+        won(0, 192, "psV")
+        runs(0, 192)
+        klist(0, 12)
+        high(0, 12)
+        prefix(3)
+        filled(3, 4)
+        scan(T.CH[:, 0:192], T.ob[:, 0:192], T.HF[:, 0:192], OP.mult, OP.add, ["ob", ("HF", 0, 192)], [("CH", 0, 192)])
+        count(0, 192, "acca")
+        won(192, 256, "psE")
+        runs(192, 256)
+        tt(T.kb[:], T.st[:, 15:256:16], T.KB[:], OP.add, ["st", "KB"], ["kb"])
+        klist(12, 16)
+        high(12, 16)
+        cp(T.kl1[:], T.kb[:], ["kb"], ["kl1"])
+        do("v", lambda v: v.tensor_reduce(T.krr[:], T.st[:, 15:256:16], AxisListType.X, OP.add), ["st"], ["krr"])
+        act(T.K[:], T.KT[:, 0:16].indirect(T.kl0[:, 0:16]), AF.Copy, ["KT", "kl0"], ["K"])
+        tt(T.D[:], T.PM[:, 0:NB].indirect(T.kl1[:, 0:16]), T.P[:, 0:NB:16], OP.subtract, ["PM", "kl1", "P"], ["D"])
+        act(T.Y[:, 0:256], T.D[:], AF.Abs, ["D"], [("Y", 0, 256)])
+        ts(T.BA[:], T.BO[:], T.krr[:], 16.0, OP.mult, OP.mult, ["BO", "krr"], ["BA"])
+        mm(psD, T.BA[:], T.ob[:], False, True, ["BA", "ob"], ["psD"])
+        for q in range(16):
+            mm(psL, T.WE[:, 15 - q:143 - q], T.Y[:, q:256:16], False, False, ["WE", ("Y", 0, 256)], ["psL"])
+        mm(psL, T.BA[:], T.o256[:, 0:16], False, True, ["BA", "o256"], ["psL"])
+        for b in ("psR", "psS"):
+            mm(T[b][:, 0:256], T.BA[:], T.o256[:], False, False, ["BA", "o256"], [b])
+            mm(T[b][:, 0:256], T.WB[:], T.Y[:, 0:256], False, True, ["WB", ("Y", 0, 256)], [b])
+
+        scan(T.CH[:, 192:256], T.ob[:, 192:256], T.HF[:, 192:256], OP.mult, OP.add, ["ob", ("HF", 192, 256), ("CH", 191, 192)],
+             [("CH", 192, 256)], ini=T.CH[:, 191:192])
+        count(192, 256, "accb")
+        ts(T.accp[:], T.acca[:], -0.5, 128.0, OP.mult, OP.add, ["acca"], ["accp"])
+        ts(T.ZF[:], T.K[:], 8.0, None, OP.is_lt, None, ["K"], ["ZF"])
+        ts(T.C[:], T.K[:], T.d16[:], None, OP.is_gt, None, ["K", "d16"], ["C"])
+        scan(T.CZ[:], T.ob[:], T.ZF[:], OP.mult, OP.add, ["ob", "ZF"], ["CZ"])
+        for c in range(2):
+            ts(T.hl[:, c:c + 1], T.accb[:, c:c + 1], -0.5, T.accp[:, c:c + 1], OP.mult, OP.add, ["accb", "accp"], [("hl", c, c + 1)])
+        act(T[PKn][:], T.Y[:, 0:272].indirect(T.hl[:, 0:2]), AF.Copy, ["Y", "hl"], [PKn])
+        send(dst, T[PKn][:], T[RXn][:], [PKn], "arr%d" % t)
+        landed(frm, "arr%d" % t, RXn)
+        for c in range(2):
+            act(T["J%d" % c][:], T.CZ[:], AF.Sign, ["CZ", "bs"], ["J%d" % c, ("accz", c, c + 1)], bias=T.bs[:, c:c + 1],
+                accum_out=T.accz[:, c:c + 1])
+        act(T.EK[:], T.ET[:, 0:16].indirect(T.kl0[:, 0:16]), AF.Copy, ["ET", "kl0"], ["EK"])
+
+        tt(psD, psD, T.C[:], OP.mult, ["psD", "C"], ["psD"])
+        ts(T.nk[:], T.nc[:], T.CZ[:, 255:256], None, OP.is_ge, None, ["nc", "CZ"], ["nk"])
+        tt(psD, psD, T.S16[:], OP.add, ["psD", "S16"], ["psD"])
+        cp(T.VI[:], psL, ["psL"], ["VI"])
+        tt(T.nd[:], T.nk[:], T.dm[:], OP.mult, ["nk", "dm"], ["nd"])
+        ts(T.VB[:], T.VI[:], 4, 4095, OP.arith_shift_right, OP.bitwise_and, ["VI"], ["VB"])
+        ts(T.zl[:], T.accz[:], -0.5, 128.0, OP.mult, OP.add, ["accz"], ["zl"])
+        cp(T.VL[:], T.VB[:], ["VB"], ["VL"])
+        act(T.OW[:], T.Y[:, 0:272].indirect(T.zl[:, 0:2]), AF.Identity, ["Y", "zl"], ["OW"], bias=-256.0)
+        act(T.vraw[:, 0:256], psR, AF.Copy, ["psR"], [("vraw", 0, 256)])
+        act(T.G32[:], T.vraw[:, 0:272].indirect(T.zl[:, 0:2]), AF.Copy, ["vraw", "zl"], ["G32"])
+        cp(spare.indirect(T.VL[:, 0:16]), T.Y[:, 0:256], ["VL", ("Y", 0, 256)], ["B"])
+
+        tt(T.t3[:], psS, T.EK[:], OP.mult, ["psS", "EK"], ["t3"])
+        tt(T.GM[:], T.G32[:], T.DM[:], OP.mult, ["G32", "DM"], ["GM"])
+        for c in range(2):
+            act(T["J%d" % c][:, 0:16], T.GM[:, 16 * c:16 * c + 16], AF.Copy, ["GM"], ["J%d" % c, ("rd", c, c + 1)],
+                accum_out=T.rd[:, c:c + 1])
+        tt(T.UI[:], psD, T.t3[:], OP.add, ["psD", "t3"], ["UI"])
+        cp(T.ri[:], T.rd[:], ["rd"], ["ri"])
+        ts(T.SI[:], T.UI[:], 4, 4095, OP.arith_shift_right, OP.bitwise_and, ["UI"], ["SI"])
+        ts(T.rb[:], T.ri[:], 4, 4095, OP.arith_shift_right, OP.bitwise_and, ["ri"], ["rb"])
+        if last:
+            cp(T.yof[:], T.SI[:], ["SI"], ["yof"])
+            dma("s", "out_yo", T.yo[:], T.yof[:], ["yof"], [])
+        else:
+            cp(T.SU[:], T.SI[:], ["SI"], ["SU"])
+        for c in range(2):
+            ts(T.OL[:, c:c + 1], T.rb[:, c:c + 1], T.nd[:, c:c + 1], None, OP.max, None, ["rb", "nd"], [("OL", c, c + 1)])
+        if not last:
+            factors()
+        tt(T.u[:], T[RXn][:], T.OW[:], OP.max, [RXn, "OW"], ["u"])
+        ts(T.w[:], T.u[:], 0.0, 256.0, OP.is_lt, OP.mult, ["u"], ["w"])
+        tt(spare.indirect(T.OL[:, 0:2]), T.u[:], T.w[:], OP.add, ["OL", "u", "w"], ["B"])
+
+    dma("y", "out_yb", T.yb[:], balls, [("B", 0, NB)], [])
+    for sem in sorted(total):
+        wait_for("g", sem, total[sem], {})

@@ -5,10 +5,29 @@ OP = AluOpType
 AF = ActivationFunctionType
 ROUNDS = 3
 NB = 4096
-DUMP = 32
-CH = 4
-CW = NB // CH
-REP = 4
+SLOTS = 64
+LEAD = 8
+VOTE = 8192
+BASE = 8 * VOTE
+OFF = 16
+RSW = 1024
+
+ORDER = """
+gather:s:0:2 gather:v:2:4 gather:s:4:8 gather:s:8:12 gather:s:12:14 gather:s:14:16 weights:0
+begin2 products tops:0:4:4:psX0 prefix:0:4 shift compare:0:4:4:psX0
+prefix:4:8 tops:4:8:4:psX1 votes:0:psV compare:4:8:4:psX1 begin3 beginT:0:16
+tops:8:12:4:psX0 prefix:8:12 votes:1:psV compare:8:12:4:psX0:0:2 run0:0:8:psV run1:0:8:psV tops:12:14:4:psX1
+compare:8:12:4:psX0:2:4 lists:0:8 marks:0:8 tops:14:16:4:psX0 votes:2:psE largest:0:8:psV compare:12:14:4:psX1
+compare:14:16:4:psX0 sums:0:8 by_k:0:8:0 votes:3:psE count:0:8:acca weights:1
+sizes:0:8:psV less:acca:2:128 masks:0:8:ps2 masks:0:8:ps3 places:0:8:ps3 beginN prefix:12:16
+run0:8:16:psE run1:8:16:psE ksum lists:8:16 kblocks marks:8:16 values:8:16 by_k:8:16:3
+adds:BA:psL:0 adds:BA:psO:0 adds:BA:ps2:0 adds:BA:ps3:0
+sums:8:16 sizes:8:16 count:8:16:accc:0:2 under:8:16:2 under:8:16:3 many:8:16:2:accc many:8:16:3:accc
+masks:8:16:ps2:1 listed:0:16 masks:8:16:ps3 places:8:16:ps3:1
+summed:acc:acca:accc first marked pack flags send zb addOT listedO addN
+VT:0:16 VB second VL own rT UJ rb SU dumped factors OL keep take
+"""
+LATE = {"rT": " first", "rb": " second", "dumped": " UJ", "OL": " SU"}
 
 SCRATCH = {}
 
@@ -18,16 +37,16 @@ def _declare(where, dtype, **shapes):
         SCRATCH[name] = (where, [128] + (n if isinstance(n, list) else [n]), dtype)
 
 
-_declare("sbuf", "bfloat16", B=NB + DUMP, P=NB, PM=NB, pat=64, WN=[16, 256], tw=256, st=256, K=256, D=256, Y=272, HF=256,
-         ZF=256, CH=256, CZ=256, J0=256, J1=256, C=256, EK=256, ob=256, o256=256, r57=256, ID=128, B1=128, BO=128, BA=128,
-         WB=128, E1=144, E2=144, E01=144, WE=144, RS=CW, KS=256, KT=16, HT=16, ET=16, iL=16, row=256, wb=1, OW=32, u=32,
-         w=32, PK0=32, PK1=32, PK2=32, RX0=32, RX1=32, RX2=32)
-_declare("sbuf", "float32", S16=256, kb=16, krr=1, acca=2, accb=2, accp=2, accz=2, vraw=272, G32=32, GM=32, rd=2, nk=2,
-         nd=2, ef=256, zu=256, t3=256, yof=256, of32=128, c16=128, cm1=128, LE=128, LS=128, NI=128, rc=1, d16=1, bs=2,
-         nc=2, dm=2, j16=16, iF=16, KB=16, rowf=256, cm=32, DM=32, wf=1)
-_declare("sbuf", "int32", SI=256, eI=256, UI=256, VI=16, VB=16, ri=2, rb=2, pI=1, rI=1, wI=1, wA=1)
-_declare("sbuf", "uint16", SU=256, kl0=16, kl1=16, hl=2, zl=2, OL=2, VL=16)
-_declare("psum", "float32", psX0=512, psX1=512, psV=512, psE=512, psD=512, psS=512, psR=512, psL=512)
+_declare("sbuf", "bfloat16", B=NB + SLOTS, P=NB, PM=OFF + NB, WN=[16, 256], Y2=528, F2=528, D=256, HZ=256, NN=256, CH=256,
+         J=[4, 256], Fb=256, ob=256, m16=256, m4k=256, cE=256, c2=256, c3=256, RS=RSW, ID=128, NI=128, B1=128, BO=128, BA=128,
+         WB=128, c28=128, Ma=128, MI=128, M3=128, LE=128, LF=128, DS=128, EV=144, E1=144, WE=144, QT=16, NT=16, HT=16, iL=16,
+         wb=1, wq=1, zb=4, fo=SLOTS, PK0=128, PK1=128, PK2=128, RX0=LEAD + 128, RX1=LEAD + 128, RX2=LEAD + 128)
+_declare("sbuf", "float16", Sh=256, L2=128)
+_declare("sbuf", "float32", st=[2, 256], C0=256, C1=272, acc=4, acca=4, accb=4, accc=4, accd=4, an=4, ks=16, kc=16, zu=256,
+         m1=256, yof=256, c16=128, LS=128, I16=128, dm=4, bs=4, rc=1, r16=1, r8=1, rh=1, rn=1, rd=1, lo=1, hi=1, wm=1, wf=1)
+_declare("sbuf", "int32", SI=256, UI=256, UJ=256, VI=16, VB=16, ri=4, rb=4, rx=4, pI=1, rI=1)
+_declare("sbuf", "uint16", SU=256, kl=[2, 16], ml=4, OL=4, VL=16)
+_declare("psum", "float32", psX0=512, psX1=512, psV=512, psE=512, ps2=512, ps3=512, psL=512, psO=512)
 
 DMAS = ["in_stk", "in_wt", "in_ball", "out_yo", "out_yb"]
 SEMAPHORES = ["qv", "qs", "qt", "qg", "ls"] + ["dma_" + d for d in DMAS] + ["arr%d" % t for t in range(ROUNDS)]
@@ -112,9 +131,9 @@ def rank_program(g, core, T, topo):
         total["ls"] = total.get("ls", 0) + len(eng)
         g.remote_dma(out, src, T.sem[sem], T.sem["ls"], pid, rid, sum(1 << e for e in eng))
 
-    def landed(frm, sem, name):
+    def landed(frm, sem, where):
         total[sem] = len(lanes_of(frm, core))
-        note("remote", sem, total[sem], [], [reg(name)])
+        note("remote", sem, total[sem], [], [where])
 
     def ts(out, in0, s1, s2, op0, op1, R, W):
         ops = (op0,) if op1 is None else (op0, op1)
@@ -135,6 +154,11 @@ def rank_program(g, core, T, topo):
     def act(out, a, f, R, W, **kw):
         do("s", lambda s: s.activation(out, a, f, **kw), R, W)
 
+    def lin(out, src, scale, bias=0.0, f=AF.Identity, cut=slice(None)):
+        cols = [x for x in (scale, bias) if isinstance(x, str)]
+        act(T[out][:], T[src][:, cut], f, [src] + cols, [out], scale=T[scale][:] if isinstance(scale, str) else scale,
+            bias=T[bias][:] if isinstance(bias, str) else bias)
+
     def mm(out, l, r, start, stop, R, W):
         do("t", lambda x: x.matmul(out, l, r, start, stop), R, W)
 
@@ -150,245 +174,285 @@ def rank_program(g, core, T, topo):
     dma("s", "in_ball", T.B[:, 0:NB], T.ball[:], [], [("B", 0, NB)])
     dma("y", "in_wt", T.wb[:], T.wt[:], [], ["wb"])
 
-    iota(T.pI[:], [[0, 1]], 0, 1, ["pI"])
-    ms(T.of32[:], 1.0, ["of32"])
-    ms(T.cm1[:], -1.0, ["cm1"])
-    ms(T.ob[:], 1.0, ["ob"])
-    ms(T.c16[:], 0.0625, ["c16"])
-    blk = [[-16, 8], [0, 16]]
-    asel(T.LE[:], T.of32[:], blk, OP.is_equal, 0.0, 0, 1, ["of32"], ["LE"])
-    asel(T.ID[:], T.ob[:, 0:128], [[-1, 128]], OP.is_equal, 0.0, 0, 1, ["ob"], ["ID"])
-    asel(T.NI[:], T.cm1[:], [[-1, 128]], OP.is_equal, 0.0, 0, 1, ["cm1"], ["NI"])
-    iota(T.rowf[:], [[16, 256]], 0, 0, ["rowf"], **small)
-    iota(T.j16[:], [[16, 16]], 0, 0, ["j16"], **small)
-    iota(T.cm[:], [[0, 2], [1, 16]], 0, 0, ["cm"], **small)
-    iota(T.KT[:], [[16, 16]], 0, 0, ["KT"], **small)
-    asel(T.E1[:], T.ob[:, 0:144], [[-16, 9], [0, 16]], OP.is_ge, 0.0, 0, 1, ["ob"], ["E1"])
-    asel(T.E2[:], T.E1[:], [[16, 9], [0, 16]], OP.is_ge, 0.0, 15, -1, ["E1"], ["E2"])
-    asel(T.E01[:], T.E2[:], [[0, 9], [1, 16]], OP.is_equal, 0.0, -15, 0, ["E2"], ["E01"])
-    asel(T.LS[:], T.c16[:], [[-1, 128]], OP.is_equal, 0.0, -1, 1, ["c16"], ["LS"])
-    asel(T.B1[:], T.ob[:, 0:128], blk, OP.is_ge, 0.0, 0, 1, ["ob"], ["B1"])
-    asel(T.BO[:], T.B1[:], [[16, 8], [0, 16]], OP.is_ge, 0.0, 15, -1, ["B1"], ["BO"])
-
-    ms(T.pat[:], 0.0, ["pat"])
-    ms(T.RS[:], 1.0, ["RS"])
-    ms(T.r57[:], 57344.0, ["r57"])
-    ms(T.RS[:, 1:CW:16], 0.0, ["RS"])
-    ms(T.KS[:], -1.0, ["KS"])
-    ms(T.pat[:, 0:64:16], 16.0, ["pat"])
-    ms(T.o256[:], 256.0, ["o256"])
-    ms(T.KS[:, 0:256:16], 100.0, ["KS"])
-    ms(T.B[:, NB:NB + DUMP], 0.0, [("B", NB, NB + DUMP)])
-    ms(T.Y[:, 256:272], -512.0, [("Y", 256, 272)])
-    ms(T.vraw[:, 256:272], 0.0, [("vraw", 256, 272)])
-    cp(T.SU[:], T.SI[:], ["SI"], ["SU"])
-
-    def early_constants():
-        ts(T.rI[:], T.pI[:], 15, None, OP.bitwise_and, None, ["pI"], ["rI"])
-        cp(T.row[:], T.rowf[:], ["rowf"], ["row"])
-        cp(T.rc[:], T.rI[:], ["rI"], ["rc"])
-        ts(T.HT[:], T.KT[:], 160.0, None, OP.is_ge, None, ["KT"], ["HT"])
-        ts(T.iF[:], T.j16[:], T.rc[:], None, OP.add, None, ["j16", "rc"], ["iF"])
-        ts(T.d16[:], T.rc[:], 16.0, None, OP.mult, None, ["rc"], ["d16"])
-        ts(T.nc[:, 0:1], T.rc[:], 0.0, None, OP.add, None, ["rc"], [("nc", 0, 1)])
-        ts(T.nc[:, 1:2], T.rc[:], 16.0, None, OP.add, None, ["rc"], [("nc", 1, 2)])
-        ts(T.KB[:], T.iF[:], 16.0, 14.0, OP.mult, OP.add, ["iF"], ["KB"])
-        ts(T.ET[:], T.KT[:], T.d16[:], None, OP.is_equal, None, ["KT", "d16"], ["ET"])
-        ts(T.iL[:], T.iF[:], 16.0, None, OP.mult, None, ["iF"], ["iL"])
-        ts(T.DM[:], T.cm[:], T.rc[:], None, OP.is_equal, None, ["cm", "rc"], ["DM"])
-        ts(T.bs[:], T.nc[:], -1.0, -0.5, OP.mult, OP.add, ["nc"], ["bs"])
-        ts(T.dm[:], T.nc[:], float(NB), None, OP.add, None, ["nc"], ["dm"])
-        cp(T.wI[:], T.wb[:], ["wb"], ["wI"])
-        ts(T.wA[:], T.wI[:], 15, None, OP.bitwise_and, None, ["wI"], ["wA"])
-        ts(T.wf[:], T.wA[:], 4096.0, None, OP.mult, None, ["wA"], ["wf"])
-
-    def late_constants():
-        ts(T.WE[:], T.E01[:], T.wf[:], None, OP.mult, None, ["E01", "wf"], ["WE"])
-        ts(T.WB[:], T.BO[:], T.wf[:], None, OP.mult, None, ["BO", "wf"], ["WB"])
-
-    balls, spare = T.B[:, 0:NB], T.B[:, 0:NB + DUMP]
-    ones, row = T.ob[0:1, 0:128], T.row[0:1, :]
-    psD, psS, psR, psL = T.psD[:, 0:256], T.psS[:, 0:256], T.psR[:, 0:256], T.psL[:, 0:16]
+    balls, spare = T.B[:, 0:NB], T.B[:, 0:NB + SLOTS]
+    ps2, ps3, psE, psL = T.ps2[:, 0:256], T.ps3[:, 0:256], T.psE[:, 0:256], T.psL[:, 0:256]
+    psO, psN = T.psO[:, 0:SLOTS], T.psX0[:, 0:4]
+    blk, half = [[-16, 8], [0, 16]], slice(0, 128)
 
     def factors():
-        ts(T.eI[:], T.SI[:], 1023, None, OP.bitwise_and, None, ["SI"], ["eI"])
-        ts(T.S16[:], T.SI[:], 16.0, None, OP.mult, None, ["SI"], ["S16"])
-        ts(T.ef[:], T.eI[:], 2.0, 1.0, OP.mult, OP.add, ["eI"], ["ef"])
-        mm(T.psE[:, 0:256], T.LE[:], T.ef[:], True, True, ["LE", "ef"], ["psE"])
+        ts(T.Sh[:], T.SU[:], -2048.0, None, OP.add, None, ["SU"], ["Sh"])
+        ts(T.Fb[:], T.SU[:], 1.0 / 1024, 191.5 + 1.0 / 2048, OP.mult, OP.add, ["SU"], ["Fb"])
+        mm(psE, T.ob[0:2, 0:128], T.cE[0:2, :], True, False, ["ob", "cE"], ["psE"])
+        mm(psE, T.L2[:], T.Sh[:], False, False, ["L2", "Sh"], ["psE"])
+        mm(psE, T.LF[:], T.Fb[:], False, True, ["LF", "Fb"], ["psE"])
 
+    ms(T.ob[:], 1.0, ["ob"])
+    iota(T.pI[:], [[0, 1]], 0, 1, ["pI"])
+    asel(T.LE[:], T.ob[:, half], blk, OP.is_equal, 0.0, 0, 1, ["ob"], ["LE"])
+    asel(T.ID[:], T.ob[:, half], [[-1, 128]], OP.is_equal, 0.0, 0, 1, ["ob"], ["ID"])
+    iota(T.QT[:], [[1, 16]], 0, 0, ["QT"], **small)
+    asel(T.B1[:], T.ob[:, half], blk, OP.is_ge, 0.0, 0, 1, ["ob"], ["B1"])
+    iota(T.C1[:], [[256, 17], [1, 16]], BASE + OFF - 1, 0, ["C1"], **small)
+    asel(T.BO[:], T.B1[:], [[16, 8], [0, 16]], OP.is_ge, 0.0, 15, -1, ["B1"], ["BO"])
+    lin("c16", "ob", 0.0625, cut=half)
+    lin("c28", "ob", 2.0 ** 28, cut=half)
+    act(T.cE[0:2, :], T.ob[0:2, :], AF.Copy, ["ob"], ["cE"])
+    act(T.c3[0:3, :], T.ob[0:3, :], AF.Copy, ["ob"], ["c3"], scale=2.0 ** 16)
+    act(T.cE[0:1, :], T.ob[0:1, :], AF.Copy, ["ob"], ["cE"], scale=4096.0 + 2048.0 * 192)
+    act(T.c3[0:2, :], T.ob[0:2, :], AF.Copy, ["ob"], ["c3"], scale=-240.0 * 2 ** 20)
+    lin("LF", "LE", -2048.0)
+    act(T.c2[0:1, :], T.ob[0:1, :], AF.Copy, ["ob"], ["c2"], scale=2.0 ** 17)
+    ms(T.RS[:], 1.0, ["RS"])
+    ts(T.rI[:], T.pI[:], 15, None, OP.bitwise_and, None, ["pI"], ["rI"])
+    ms(T.EV[:], 0.0, ["EV"])
+    cp(T.rc[:], T.rI[:], ["rI"], ["rc"])
+    ms(T.RS[:, 1:RSW:16], 0.0, ["RS"])
+    ts(T.L2[:], T.LE[:], 2.0, None, OP.mult, None, ["LE"], ["L2"])
+    cp(T.SU[:], T.SI[:], ["SI"], ["SU"])
+    ts(T.UJ[:], T.SI[:], 16.0, None, OP.mult, None, ["SI"], ["UJ"])
     factors()
-    early_constants()
-
+    ts(T.hi[:], T.rc[:], 8.0, 512.0, OP.is_ge, OP.mult, ["rc"], ["hi"])
+    ts(T.lo[:], T.rc[:], 8.0, None, OP.is_lt, None, ["rc"], ["lo"])
+    ms(T.Y2[:], 0.0, ["Y2"])
+    ms(T.F2[:], 0.0, ["F2"])
+    ms(T.E1[:], 0.0, ["E1"])
+    ms(T.B[:, NB:NB + SLOTS], 0.0, [("B", NB, NB + SLOTS)])
+    ms(T.PM[:, 0:OFF], 255.0, [("PM", 0, OFF)])
+    ms(T.F2[:, 512:528], 1.0, ["F2"])
+    ms(T.kc[:], -BASE - 16.0, ["kc"])
+    ts(T.HT[:], T.QT[:], 10.0, T.lo[:], OP.is_ge, OP.mult, ["QT", "lo"], ["HT"])
+    ts(T.NT[:], T.QT[:], T.rc[:], None, OP.is_le, None, ["QT", "rc"], ["NT"])
+    ts(T.rh[:], T.rc[:], 0.5, None, OP.add, None, ["rc"], ["rh"])
+    ts(T.HT[:, 0:1], T.rc[:], 8.0, None, OP.is_ge, None, ["rc"], ["HT"])
+    ts(T.rn[:], T.rc[:], 16.0, 16.0 * NB, OP.mult, OP.add, ["rc"], ["rn"])
     for t in range(ROUNDS):
+        ms(T["RX%d" % t][:, 0:LEAD], 0.0, [("RX%d" % t, 0, LEAD)])
+    ts(T.EV[:, 15:143:16], T.BO[:, 0:128:16], float(VOTE), None, OP.mult, None, ["BO"], ["EV"])
+    cp(T.E1[:, 15:143:16], T.BO[:, 0:128:16], ["BO"], ["E1"])
+    ms(T.m16[:], -16.0, ["m16"])
+    ms(T.m4k[:], -4096.0, ["m4k"])
+    lin("r16", "rc", 16.0)
+    lin("MI", "ID", -2.0 ** 24)
+    lin("NI", "ID", -1.0)
+    lin("C1", "C1", 1.0, "r16")
+    lin("iL", "QT", 256.0, "r16")
+    act(T.C1[:, 0:272:16], T.C1[:, 0:272:16], AF.Identity, ["C1"], ["C1"], bias=-240.0)
+    lin("r8", "hi", -1.0 / 64, "rh")
+    lin("rd", "hi", -65536.0, "rn")
+    act(T.C1[:, 1:272:16], T.ob[:, 0:17], AF.Copy, ["ob"], ["C1"], scale=float(BASE))
+    lin("DS", "ID", "hi")
+    lin("bs", "QT", 8.0, "r8", cut=slice(0, 4))
+    lin("dm", "QT", 256.0, "rd", cut=slice(0, 4))
+    asel(T.LS[:], T.c16[:], [[-1, 128]], OP.is_equal, 0.0, -1, 1, ["c16"], ["LS"])
+    iota(T.c3[0:1, :], [[16, 256]], 0, 0, ["c3"], **small)
+    iota(T.C0[:], [[0, 16], [1, 16]], BASE - 1, 0, ["C0"], **small)
+    asel(T.Ma[:], T.c28[:], [[-1, 128]], OP.is_equal, 0.0, 0, 1, ["c28"], ["Ma"])
+    iota(T.C0[:, 0:256:16], [[0, 16]], BASE + 15, 0, ["C0"], **small)
+    asel(T.M3[:], T.Ma[:], [[1, 128]], OP.not_equal, -2.0 ** 28, -1, -1, ["Ma"], ["M3"])
+    asel(T.I16[:], T.c16[:], [[-1, 128]], OP.is_equal, 0.0, 0, 1, ["c16"], ["I16"])
+    asel(T.M3[:, 0:128:16], T.M3[:, 0:128:16], [[-16, 8]], OP.not_equal, 0.0, 1, 1, ["M3"], ["M3"])
+
+    def weights(part):
+        if part == 0:
+            lin("wq", "wb", 1.0 / 16, 191.5 + 1.0 / 32)
+            lin("wm", "wq", -65536.0, 65536.0 * 192)
+            lin("wf", "wb", 4096.0, "wm")
+        else:
+            lin("WB", "BO", "wf")
+            lin("WE", "E1", "wf")
+
+    def throw(t):
         last = t == ROUNDS - 1
         n = len(T.cores)
         dst, frm = T.cores[(rank + t + 1) % n], T.cores[(rank - t - 1) % n]
-        PKn, RXn = "PK%d" % t, "RX%d" % t
+        PK, RX = "PK%d" % t, "RX%d" % t
 
-        def part(name, c):
-            return (name, CW * c, CW * c + CW)
-
-        def gather(q, a, b):
-            out, off = T.P[:, 16 * a:16 * b], T.SU[:, a:b]
-            R, W = [("B", 0, NB), ("SU", a, b)], [("P", 16 * a, 16 * b)]
+        def gather(q, j, e):
+            out, off = T.P[:, 256 * j:256 * e], T.SU[:, 16 * j:16 * e]
+            R, W = [("B", 0, NB), ("SU", 16 * j, 16 * e)], [("P", 256 * j, 256 * e)]
             if q == "s":
                 act(out, balls.indirect(off), AF.Copy, R, W)
             else:
                 cp(out, balls.indirect(off), R, W)
 
-        def tops(c):
-            b = "psX%d" % (c % 2)
-            for r in range(REP):
-                mm(T[b][:, r:64 * REP:REP], T.ID[:], T.P[:, CW * c:CW * c + CW:16], True, True, ["ID", part("P", c)], [b])
+        def tops(j, e, rep, b):
+            for r in range(rep):
+                mm(T[b][:, r:16 * (e - j) * rep:rep], T.ID[:], T.P[:, 256 * j:256 * e:16], True, True,
+                   ["ID", ("P", 256 * j, 256 * e)], [b])
 
-        def compare(c):
-            b, s = "psX%d" % (c % 2), 16 // REP
-            for d in range(s):
-                tt(T.WN[:, 4 * c:4 * c + 4, d:256:s], T.P[:, CW * c + d:CW * c + CW:s], T[b][:, 0:64 * REP],
-                   OP.is_lt, [part("P", c), b], [part("WN", c)], waw=False)
+        def compare(j, e, rep, b, first=0, end=16):
+            s = 16 // rep
+            for d in range(first, min(end, s)):
+                tt(T.WN[:, j:e, d:256:s], T.P[:, 256 * j + d:256 * e:s], T[b][:, 0:16 * (e - j) * rep],
+                   OP.is_lt, [("P", 256 * j, 256 * e), b], [("WN", 256 * j, 256 * e)], waw=False)
 
-        def votes(c, b):
-            mm(T[b][:, 64 * c:64 * c + 64], ones, T.pat[0:1, :], True, False, ["ob", "pat"], [b])
+        def votes(c, b, first=0, end=16):
+            for q in range(first, end):
+                mm(T[b][:, 64 * c:64 * c + 64], T.EV[:, 15 - q:143 - q], T.WN[:, 4 * c:4 * c + 4, 16 * q:16 * q + 16],
+                   q == 0, q == 15, ["EV", ("WN", 1024 * c, 1024 * c + 1024)], [b])
+
+        def prefix(j, e):
+            scan(T.PM[:, OFF + 256 * j:OFF + 256 * e], T.RS[:, 0:256 * (e - j)], T.P[:, 256 * j:256 * e], OP.mult, OP.max,
+                 ["RS", ("P", 256 * j, 256 * e)], [("PM", OFF + 256 * j, OFF + 256 * e)])
+
+        def run(i, C, ini, j, e, b):
+            back = slice(16 * e - 1, 16 * j - 1 if j else None, -1)
+            scan(T.st[:, i, back], T[b][:, back], T[C][:, back], OP.min, OP.max, [b, C],
+                 [("st", 256 * i + 16 * j, 256 * i + 16 * e)], ini=ini)
+
+        def lists(j, e):
+            ts(T.kl[:, :, j:e], T.st[:, :, 16 * j + 1:16 * e:16], -float(BASE), None, OP.add, None,
+               [("st", 16 * j, 16 * e), ("st", 256 + 16 * j, 256 + 16 * e)], [("kl", j, e), ("kl", 16 + j, 16 + e)])
+
+        def by_k(j, e, a):
+            act(T.NN[:, 16 * j:16 * e], T.NT[:, 0:16].indirect(T.kl[:, 0, j:e]), AF.Copy, ["NT", ("kl", j, e)],
+                [("NN", 16 * j, 16 * e), ("an", a, a + 1)], accum_out=T.an[:, a:a + 1])
+
+        def values(j, e):
+            tt(T.D[:, 16 * j:16 * e], T.PM[:, 0:OFF + 256 * e].indirect(T.kl[:, 1, j:e]), T.P[:, 256 * j:256 * e:16],
+               OP.subtract, [("PM", 0, OFF + 256 * e), ("kl", 16 + j, 16 + e), ("P", 256 * j, 256 * e)], [("D", 16 * j, 16 * e)])
+
+        def largest(j, e, b):
+            act(T.D[:, 16 * j:16 * e], T.PM[:, 0:OFF + 256 * e].indirect(T.kl[:, 1, j:e]), AF.Copy,
+                [("PM", 0, OFF + 256 * e), ("kl", 16 + j, 16 + e)], [("D", 16 * j, 16 * e)])
+            mm(T[b][:, 16 * j:16 * e], T.NI[:], T.P[:, 256 * j:256 * e:16], True, False, ["NI", ("P", 256 * j, 256 * e)], [b])
+            mm(T[b][:, 16 * j:16 * e], T.ID[:], T.D[:, 16 * j:16 * e], False, True, ["ID", ("D", 16 * j, 16 * e)], [b])
+
+        def sizes(j, e, b="D"):
+            act(T.Y2[:, 32 * j:32 * e:2], T[b][:, 16 * j:16 * e], AF.Abs, [(b, 16 * j, 16 * e)], [("Y2", 32 * j, 32 * e)])
+
+        def listed(j, e):
             for q in range(16):
-                mm(T[b][:, 64 * c:64 * c + 64], T.E01[:, 15 - q:143 - q], T.WN[:, 4 * c:4 * c + 4, 16 * q:16 * q + 16],
-                   False, q == 15, ["E01", part("WN", c)], [b])
+                mm(T.psL[:, j:e], T.WE[:, 15 - q:143 - q], T.Y2[:, 32 * j + 2 * q:32 * e:32], False, q == 15 and e == 16,
+                   ["WE", ("Y2", 32 * j, 32 * e)], ["psL"])
 
-        def prefix(c):
-            scan(T.PM[:, CW * c:CW * c + CW], T.RS[:], T.P[:, CW * c:CW * c + CW], OP.mult, OP.max,
-                 ["RS", part("P", c)], [part("PM", c)])
+        def listed_o():
+            for q in range(16):
+                mm(T.psO[:, 0:4], T.WE[:, 15 - q:143 - q], T[PK][:, q:SLOTS:16], False, q == 15, ["WE", (PK, 0, SLOTS)], ["psO"])
 
-        def filled(c, e):
-            a, e = CW * c, CW * e
-            act(T.PM[:, a:e:16], T.P[:, a:e:16], AF.Identity, [("P", a, e)], [("PM", a, e)], bias=255.0, scale=0.0)
+        def masks(j, e, b, stop=0):
+            a, e, by = 16 * j, 16 * e, {"ps2": "MI", "ps3": "M3"}[b]
+            mm(T[b][:, a:e], T[by][:], T.NN[:, a:e], False, bool(stop), [by, ("NN", a, e)], [b])
 
-        def won(a, e, b):
-            ts(T.tw[:, a:e], T[b][:, a:e], 9.0, 16.0, OP.is_ge, OP.mult, [b], [("tw", a, e)])
+        def places(j, e, b, stop=0):
+            mm(T[b][:, 16 * j:16 * e], T.WB[:], T.Y2[:, 32 * j:32 * e:2], False, bool(stop), ["WB", ("Y2", 32 * j, 32 * e)], [b])
 
-        def runs(a, e):
-            scan(T.st[:, a:e], T.KS[:, a:e], T.tw[:, a:e], OP.add, OP.min, ["KS", ("tw", a, e)], [("st", a, e)])
+        def marks(j, e):
+            act(T.HZ[:, 16 * j:16 * e], T.HT[:, 0:16].indirect(T.kl[:, 0, j:e]), AF.Copy, ["HT", ("kl", j, e)],
+                [("HZ", 16 * j, 16 * e)])
 
-        def klist(j, e):
-            ts(T.kl0[:, j:e], T.st[:, 16 * j + 15:16 * e:16], 14.0, None, OP.add, None, [("st", 16 * j, 16 * e)], [("kl0", j, e)])
+        def sums(j, e):
+            a, e = 16 * j, 16 * e
+            scan(T.CH[:, a:e], T.ob[:, a:e], T.HZ[:, a:e], OP.mult, OP.add,
+                 ["ob", ("HZ", a, e)] + ([("CH", a - 1, a)] if a else []), [("CH", a, e)], ini=T.CH[:, a - 1:a] if a else 0.0)
 
-        def high(j, e):
-            act(T.HF[:, 16 * j:16 * e], T.HT[:, 0:16].indirect(T.kl0[:, j:e]), AF.Copy, ["HT", ("kl0", j, e)], [("HF", 16 * j, 16 * e)])
+        def adds(ba, b, stop):
+            out, by = {"ps2": (ps2, T.m16[:]), "ps3": (ps3, T.m4k[:]), "psL": (T.psL[:, 0:16], T.m4k[:, 0:16]),
+                       "psO": (T.psO[:, 0:4], T.m4k[:, 0:4])}[b]
+            mm(out, T[ba][:], by, b == "psO" and ba == "BA", bool(stop), [ba, "m16", "m4k"], [b])
 
-        def count(a, e, acc):
-            for c in range(2):
-                act(T["J%d" % c][:, a:e], T.CH[:, a:e], AF.Sign, [("CH", a, e), "bs"], ["J%d" % c, (acc, c, c + 1)],
-                    bias=T.bs[:, c:c + 1], accum_out=T[acc][:, c:c + 1])
+        def count(j, e, acc, first=0, end=4):
+            a, e = 16 * j, 16 * e
+            for c in range(first, end):
+                act(T.J[:, c, a:e], T.CH[:, a:e], AF.Sign, [("CH", a, e), "bs"], [("J", 256 * c + a, 256 * c + e), (acc, c, c + 1)],
+                    bias=T.bs[:, c:c + 1], scale=-1.0, accum_out=T[acc][:, c:c + 1])
 
-        gather("s", 0, 32)
-        gather("v", 32, 64)
-        gather("s", 64, 128)
-        gather("s", 128, 192)
-        gather("s", 192, 256)
-        tops(0)
-        compare(0)
-        mm(psD, T.NI[:], T.S16[:], True, False, ["NI", "S16"], ["psD"])
-        mm(psD, ones, T.r57[0:1, :], False, False, ["ob", "r57"], ["psD"])
-        mm(psR, ones, row, True, False, ["ob", "row"], ["psR"])
-        mm(psL, T.ID[:], T.iL[:], True, False, ["ID", "iL"], ["psL"])
-        tops(1)
-        votes(0, "psV")
-        tt(T.zu[:], T.S16[:], T.psE[:, 0:256], OP.mult, ["S16", "psE"], ["zu"])
-        tops(2)
-        prefix(0)
-        compare(1)
-        votes(1, "psV")
-        mm(psD, T.LS[:], T.zu[:], False, False, ["LS", "zu"], ["psD"])
-        if t == 0:
-            late_constants()
-        tops(3)
-        prefix(1)
-        compare(2)
-        votes(2, "psV")
-        prefix(2)
-        filled(0, 3)
-        compare(3)
-        votes(3, "psE")
-        mm(psS, T.NI[:], T.S16[:], True, False, ["NI", "S16"], ["psS"])
-        mm(psS, ones, row, False, False, ["ob", "row"], ["psS"])
+        def pick(out, a, e, b):
+            scan(T[out][:, a:e], T.RD[:, a:e], T[b][:, a:e], OP.add, OP.max, ["RD", b], [(out, a, e)])
 
-        won(0, 192, "psV")
-        runs(0, 192)
-        klist(0, 12)
-        high(0, 12)
-        prefix(3)
-        filled(3, 4)
-        scan(T.CH[:, 0:192], T.ob[:, 0:192], T.HF[:, 0:192], OP.mult, OP.add, ["ob", ("HF", 0, 192)], [("CH", 0, 192)])
-        count(0, 192, "acca")
-        won(192, 256, "psE")
-        runs(192, 256)
-        tt(T.kb[:], T.st[:, 15:256:16], T.KB[:], OP.add, ["st", "KB"], ["kb"])
-        klist(12, 16)
-        high(12, 16)
-        cp(T.kl1[:], T.kb[:], ["kb"], ["kl1"])
-        do("v", lambda v: v.tensor_reduce(T.krr[:], T.st[:, 15:256:16], AxisListType.X, OP.add), ["st"], ["krr"])
-        act(T.K[:], T.KT[:, 0:16].indirect(T.kl0[:, 0:16]), AF.Copy, ["KT", "kl0"], ["K"])
-        tt(T.D[:], T.PM[:, 0:NB].indirect(T.kl1[:, 0:16]), T.P[:, 0:NB:16], OP.subtract, ["PM", "kl1", "P"], ["D"])
-        act(T.Y[:, 0:256], T.D[:], AF.Abs, ["D"], [("Y", 0, 256)])
-        ts(T.BA[:], T.BO[:], T.krr[:], 16.0, OP.mult, OP.mult, ["BO", "krr"], ["BA"])
-        mm(psD, T.BA[:], T.ob[:], False, True, ["BA", "ob"], ["psD"])
-        for q in range(16):
-            mm(psL, T.WE[:, 15 - q:143 - q], T.Y[:, q:256:16], False, False, ["WE", ("Y", 0, 256)], ["psL"])
-        mm(psL, T.BA[:], T.o256[:, 0:16], False, True, ["BA", "o256"], ["psL"])
-        for b in ("psR", "psS"):
-            mm(T[b][:, 0:256], T.BA[:], T.o256[:], False, False, ["BA", "o256"], [b])
-            mm(T[b][:, 0:256], T.WB[:], T.Y[:, 0:256], False, True, ["WB", ("Y", 0, 256)], [b])
+        def begin_list(j, e, b):
+            a, e = 16 * j, 16 * e
+            mm(T[b][:, a:e], T.MI[:], T.MO[:, a:e], True, False, ["MI", "MO"], [b])
+            mm(T[b][:, a:e], T.ob[0:1, 0:128], T.c3[0:1, a:e], False, False, ["ob", "c3"], [b])
 
-        scan(T.CH[:, 192:256], T.ob[:, 192:256], T.HF[:, 192:256], OP.mult, OP.add, ["ob", ("HF", 192, 256), ("CH", 191, 192)],
-             [("CH", 192, 256)], ini=T.CH[:, 191:192])
-        count(192, 256, "accb")
-        ts(T.accp[:], T.acca[:], -0.5, 128.0, OP.mult, OP.add, ["acca"], ["accp"])
-        ts(T.ZF[:], T.K[:], 8.0, None, OP.is_lt, None, ["K"], ["ZF"])
-        ts(T.C[:], T.K[:], T.d16[:], None, OP.is_gt, None, ["K", "d16"], ["C"])
-        scan(T.CZ[:], T.ob[:], T.ZF[:], OP.mult, OP.add, ["ob", "ZF"], ["CZ"])
-        for c in range(2):
-            ts(T.hl[:, c:c + 1], T.accb[:, c:c + 1], -0.5, T.accp[:, c:c + 1], OP.mult, OP.add, ["accb", "accp"], [("hl", c, c + 1)])
-        act(T[PKn][:], T.Y[:, 0:272].indirect(T.hl[:, 0:2]), AF.Copy, ["Y", "hl"], [PKn])
-        send(dst, T[PKn][:], T[RXn][:], [PKn], "arr%d" % t)
-        landed(frm, "arr%d" % t, RXn)
-        for c in range(2):
-            act(T["J%d" % c][:], T.CZ[:], AF.Sign, ["CZ", "bs"], ["J%d" % c, ("accz", c, c + 1)], bias=T.bs[:, c:c + 1],
-                accum_out=T.accz[:, c:c + 1])
-        act(T.EK[:], T.ET[:, 0:16].indirect(T.kl0[:, 0:16]), AF.Copy, ["ET", "kl0"], ["EK"])
+        def pass_on():
+            send(dst, T[PK][:], T[RX][:, LEAD:LEAD + 128], [PK], "arr%d" % t)
+            landed(frm, "arr%d" % t, (RX, LEAD, LEAD + 128))
 
-        tt(psD, psD, T.C[:], OP.mult, ["psD", "C"], ["psD"])
-        ts(T.nk[:], T.nc[:], T.CZ[:, 255:256], None, OP.is_ge, None, ["nc", "CZ"], ["nk"])
-        tt(psD, psD, T.S16[:], OP.add, ["psD", "S16"], ["psD"])
-        cp(T.VI[:], psL, ["psL"], ["VI"])
-        tt(T.nd[:], T.nk[:], T.dm[:], OP.mult, ["nk", "dm"], ["nd"])
-        ts(T.VB[:], T.VI[:], 4, 4095, OP.arith_shift_right, OP.bitwise_and, ["VI"], ["VB"])
-        ts(T.zl[:], T.accz[:], -0.5, 128.0, OP.mult, OP.add, ["accz"], ["zl"])
-        cp(T.VL[:], T.VB[:], ["VB"], ["VL"])
-        act(T.OW[:], T.Y[:, 0:272].indirect(T.zl[:, 0:2]), AF.Identity, ["Y", "zl"], ["OW"], bias=-256.0)
-        act(T.vraw[:, 0:256], psR, AF.Copy, ["psR"], [("vraw", 0, 256)])
-        act(T.G32[:], T.vraw[:, 0:272].indirect(T.zl[:, 0:2]), AF.Copy, ["vraw", "zl"], ["G32"])
-        cp(spare.indirect(T.VL[:, 0:16]), T.Y[:, 0:256], ["VL", ("Y", 0, 256)], ["B"])
+        def stacks():
+            if last:
+                ts(T.yof[:], T.UJ[:], 0.0625, None, OP.mult, None, ["UJ"], ["yof"])
+                dma("s", "out_yo", T.yo[:], T.yof[:], ["yof"], [])
+            else:
+                ts(T.SU[:], T.UJ[:], 0.0625, None, OP.mult, None, ["UJ"], ["SU"])
 
-        tt(T.t3[:], psS, T.EK[:], OP.mult, ["psS", "EK"], ["t3"])
-        tt(T.GM[:], T.G32[:], T.DM[:], OP.mult, ["G32", "DM"], ["GM"])
-        for c in range(2):
-            act(T["J%d" % c][:, 0:16], T.GM[:, 16 * c:16 * c + 16], AF.Copy, ["GM"], ["J%d" % c, ("rd", c, c + 1)],
-                accum_out=T.rd[:, c:c + 1])
-        tt(T.UI[:], psD, T.t3[:], OP.add, ["psD", "t3"], ["UI"])
-        cp(T.ri[:], T.rd[:], ["rd"], ["ri"])
-        ts(T.SI[:], T.UI[:], 4, 4095, OP.arith_shift_right, OP.bitwise_and, ["UI"], ["SI"])
-        ts(T.rb[:], T.ri[:], 4, 4095, OP.arith_shift_right, OP.bitwise_and, ["ri"], ["rb"])
+        def take():
+            tt(spare.indirect(T.OL[:, 0:4]), T.fo[:], T[RX][:, 0:SLOTS], OP.add, ["OL", "fo", RX], ["B"])
+            if last:
+                dma("y", "out_yb", T.yb[:], balls, [("B", 0, NB)], [])
+
+        def place(out, src):
+            ts(T[out][:], T[src][:], 4, 4095, OP.arith_shift_right, OP.bitwise_and, [src], [out])
+
+        steps = {
+            "gather": gather, "tops": tops, "compare": compare, "votes": votes, "prefix": prefix, "lists": lists, "by_k": by_k,
+            "values": values, "sizes": sizes, "masks": masks, "places": places, "marks": marks, "sums": sums, "count": count,
+            "beginL": begin_list, "send": pass_on, "SU": stacks,
+            "factors": lambda: None if last else factors(),
+            "products": lambda: tt(T.zu[:], T.UJ[:], psE, OP.mult, ["UJ", "psE"], ["zu"]),
+            "begin2": lambda: mm(ps2, T.ob[0:1, 0:128], T.c2[0:1, :], True, False, ["ob", "c2"], ["ps2"]),
+            "begin3": lambda: mm(ps3, T.ob[0:3, 0:128], T.c3[0:3, :], True, False, ["ob", "c3"], ["ps3"]),
+            "beginO": lambda: mm(psO, T.MI[:], T.MO[:, 0:SLOTS], True, False, ["MI", "MO"], ["psO"]),
+            "beginN": lambda: mm(psN, T.I16[:], T.dm[:], True, False, ["I16", "dm"], ["psX0"]),
+            "shift": lambda: mm(ps2, T.LS[:], T.zu[:], False, False, ["LS", "zu"], ["ps2"]),
+            "run0": lambda j, e, b: run(0, "C0", BASE + 15.0, j, e, b),
+            "run1": lambda j, e, b: run(1, "C1", T.C1[:, 16 * e:16 * e + 1], j, e, b),
+            "both": lambda: act(T.an[:, 2:3], T.an[:, 0:1], AF.Identity, [("an", 0, 2)], [("an", 2, 3)], bias=T.an[:, 1:2]),
+            "blocks": lambda ba, a: act(T[ba][:], T.BO[:], AF.Copy, ["BO", ("an", a, a + 1)], [ba], scale=T.an[:, a:a + 1]),
+            "adds": adds, "weights": lambda part: None if t else weights(part),
+            "ksum": lambda: scan(T.ks[:], T.kc[:], T.st[:, 0, 1:256:16], OP.add, OP.add, ["kc", ("st", 0, 256)], ["ks"]),
+            "kblocks": lambda: ts(T.BA[:], T.BO[:], T.ks[:, 15:16], -1.0, OP.mult, OP.mult, ["BO", "ks"], ["BA"]),
+            "under": lambda j, e, c: ts(T.J[:, c, 16 * j:16 * e], T.CH[:, 16 * j:16 * e], T.bs[:, c:c + 1], 2.0, OP.is_lt, OP.mult,
+                                        [("CH", 16 * j, 16 * e), "bs"], [("J", 256 * c + 16 * j, 256 * c + 16 * e)]),
+            "many": lambda j, e, c, acc: do("v", lambda v: v.tensor_reduce(T[acc][:, c:c + 1], T.J[:, c, 16 * j:16 * e], AxisListType.X, OP.add),
+                                            [reg(("J", 256 * c + 16 * j, 256 * c + 16 * e))], [(acc, c, c + 1)]),
+            "less": lambda acc, c, n: act(T[acc][:, c:4], T[acc][:, c:4], AF.Identity, [acc], [acc], bias=-float(n)),
+            "addL": lambda j, e, b: mm(T[b][:, 16 * j:16 * e], T.BA[:], T.m4k[:, 16 * j:16 * e], False, True, ["BA", "m4k"], [b]),
+            "largest": largest, "listed": listed, "listedO": listed_o,
+            "beginT": lambda j, e: mm(T.psL[:, j:e], T.ID[:], T.iL[:, j:e], True, False, ["ID", "iL"], ["psL"]),
+            "addT": lambda j, e: mm(T.psL[:, j:e], T.BA[:], T.m4k[:, j:e], False, True, ["BA", "m4k"], ["psL"]),
+            "VT": lambda j, e: cp(T.VI[:, j:e], T.psL[:, j:e], ["psL"], [("VI", j, e)]),
+            "beginOT": lambda: mm(T.psO[:, 0:4], T.BA[:], T.m4k[:, 0:4], True, False, ["BA", "m4k"], ["psO"]),
+            "addOT": lambda: mm(T.psO[:, 0:4], T.ID[:], T.zb[:], False, False, ["ID", "zb"], ["psO"]),
+            "rT": lambda: cp(T.ri[:], T.psO[:, 0:4], ["psO"], ["ri"]),
+            "marked4": lambda: [ts(T.ml[:, c:c + 1], T.accb[:, c:c + 1], T.acca[:, c:c + 1], 256.0, OP.add, OP.add,
+                                   ["acca", "accb"], [("ml", c, c + 1)]) for c in range(4)],
+            "add2": lambda: mm(ps2, T.BA[:], T.m16[:], False, True, ["BA", "m16"], ["ps2"]),
+            "add3": lambda: mm(ps3, T.BA[:], T.m4k[:], False, True, ["BA", "m4k"], ["ps3"]),
+            "addO": lambda: mm(psO, T.BA[:], T.m4k[:, 0:SLOTS], False, False, ["BA", "m4k"], ["psO"]),
+            "addN": lambda: mm(psN, T.DS[:], T.zb[:], False, True, ["DS", "zb"], ["psX0"]),
+            "placesO": lambda: mm(psO, T.WB[:], T[PK][:, 0:SLOTS], False, True, ["WB", (PK, 0, SLOTS)], ["psO"]),
+            "pick": lambda j, e, b: pick("dg", 16 * j, 16 * e, b),
+            "pickO": lambda: pick("do", 0, SLOTS, "psO"),
+            "VI": lambda j, e: cp(T.VI[:, j:e], T.dg[:, 16 * j + 15:16 * e:16], [("dg", 16 * j, 16 * e)], [("VI", j, e)]),
+            "VB": lambda: place("VB", "VI"),
+            "VL": lambda: cp(T.VL[:], T.VB[:], ["VB"], ["VL"]),
+            "own": lambda: cp(spare.indirect(T.VL[:, 0:16]), T.Y2[:, 0:512:2], ["VL", "Y2"], ["B"]),
+            "first": lambda: tt(T.m1[:], ps2, T.UJ[:], OP.max, ["ps2", "UJ"], ["m1"]),
+            "second": lambda: tt(T.UI[:], ps3, T.m1[:], OP.max, ["ps3", "m1"], ["UI"]),
+            "UJ": lambda: ts(T.UJ[:], T.UI[:], 0xFFF0, None, OP.bitwise_and, None, ["UI"], ["UJ"]),
+            "summed": lambda o, a, b: tt(T[o][:], T[a][:], T[b][:], OP.add, [a, b], [o]),
+            "marked": lambda: ts(T.ml[:], T.acc[:], 256.0, None, OP.add, None, ["acc"], ["ml"]),
+            "pack": lambda: act(T[PK][:, 0:SLOTS], T.Y2[:, 0:528].indirect(T.ml[:, 0:4]), AF.Copy, ["Y2", "ml"], [(PK, 0, SLOTS)]),
+            "flags": lambda: act(T[PK][:, SLOTS:128], T.F2[:, 0:528].indirect(T.ml[:, 0:4]), AF.Copy, ["F2", "ml"],
+                                 [(PK, SLOTS, 128)]),
+            "zb": lambda: lin("zb", "acc", 8.0, 2048.0),
+            "ri": lambda: tt(T.ri[:], T.do[:, 15:SLOTS:16], T.zb[:], OP.add, ["do", "zb"], ["ri"]),
+            "rb": lambda: place("rb", "ri"),
+            "dumped": lambda: tt(T.rx[:], psN, T.rb[:], OP.max, ["psX0", "rb"], ["rx"]),
+            "OL": lambda: cp(T.OL[:], T.rx[:], ["rx"], ["OL"]),
+            "keep": lambda: tt(T.fo[:], T[RX][:, SLOTS:128], T[PK][:, 0:SLOTS], OP.mult, [RX, (PK, 0, SLOTS)], ["fo"]),
+            "take": take,
+        }
+        words = ORDER.split()
         if last:
-            cp(T.yof[:], T.SI[:], ["SI"], ["yof"])
-            dma("s", "out_yo", T.yo[:], T.yof[:], ["yof"], [])
-        else:
-            cp(T.SU[:], T.SI[:], ["SI"], ["SU"])
-        for c in range(2):
-            ts(T.OL[:, c:c + 1], T.rb[:, c:c + 1], T.nd[:, c:c + 1], None, OP.max, None, ["rb", "nd"], [("OL", c, c + 1)])
-        if not last:
-            factors()
-        tt(T.u[:], T[RXn][:], T.OW[:], OP.max, [RXn, "OW"], ["u"])
-        ts(T.w[:], T.u[:], 0.0, 256.0, OP.is_lt, OP.mult, ["u"], ["w"])
-        tt(spare.indirect(T.OL[:, 0:2]), T.u[:], T.w[:], OP.add, ["OL", "u", "w"], ["B"])
+            words = " ".join(w + LATE.get(w, "") for w in words if " " + w not in LATE.values()).split()
+        for word in words:
+            name, *args = word.split(":")
+            steps[name](*[int(a) if a.isdigit() else a for a in args])
 
-    dma("y", "out_yb", T.yb[:], balls, [("B", 0, NB)], [])
+    for t in range(ROUNDS):
+        throw(t)
+
     for sem in sorted(total):
         wait_for("g", sem, total[sem], {})

@@ -1,33 +1,29 @@
 import numpy as np
-from concourse.mybir import AluOpType, AxisListType, ActivationFunctionType
+from concourse.mybir import AluOpType, ActivationFunctionType
 
 OP = AluOpType
 AF = ActivationFunctionType
 ROUNDS = 3
 NB = 4096
-SLOTS = 64
-LEAD = 8
+SLOTS = 32
 VOTE = 8192
 BASE = 8 * VOTE
 OFF = 16
 RSW = 1024
 
 ORDER = """
-gather:s:0:2 gather:v:2:4 gather:s:4:8 gather:s:8:12 gather:s:12:14 gather:s:14:16 weights:0
-begin2 products tops:0:4:4:psX0 prefix:0:4 shift compare:0:4:4:psX0
-prefix:4:8 tops:4:8:4:psX1 votes:0:psV compare:4:8:4:psX1 begin3 beginT:0:16
-tops:8:12:4:psX0 prefix:8:12 votes:1:psV compare:8:12:4:psX0:0:2 run0:0:8:psV run1:0:8:psV tops:12:14:4:psX1
-compare:8:12:4:psX0:2:4 lists:0:8 marks:0:8 tops:14:16:4:psX0 votes:2:psE largest:0:8:psV compare:12:14:4:psX1
-compare:14:16:4:psX0 sums:0:8 by_k:0:8:0 votes:3:psE count:0:8:acca weights:1
-sizes:0:8:psV less:acca:2:128 masks:0:8:ps2 masks:0:8:ps3 places:0:8:ps3 beginN prefix:12:16
-run0:8:16:psE run1:8:16:psE ksum lists:8:16 kblocks marks:8:16 values:8:16 by_k:8:16:3
-adds:BA:psL:0 adds:BA:psO:0 adds:BA:ps2:0 adds:BA:ps3:0
-sums:8:16 sizes:8:16 count:8:16:accc:0:2 under:8:16:2 under:8:16:3 many:8:16:2:accc many:8:16:3:accc
-masks:8:16:ps2:1 listed:0:16 masks:8:16:ps3 places:8:16:ps3:1
-summed:acc:acca:accc first marked pack flags send zb addOT listedO addN
-VT:0:16 VB second VL own rT UJ rb SU dumped factors OL keep take
+begun gather:s:0:2 gather:v:2:4 gather:s:4:8 gather:s:8:12 gather:s:12:14 gather:s:14:16 weights:0
+begin2 products tops:0:4:8:psX0 prefix:0:4 shift halves:0:4:psX0
+tops:4:8:8:psX1 prefix:4:8 votes:0:psV halves:4:8:psX1 begin3 beginL
+tops:8:12:8:psX0 prefix:8:12 votes:1:psV halves:8:12:psX0:0:1 run0:0:8:psV run1:0:8:psV tops:12:14:4:psX1
+halves:8:12:psX0:1:4 lists:0:8 by_k:H:s:0:8 by_k:Z:s:0:8 tops:14:16:4:psX0 votes:2:psE compare:12:14:4:psX1
+compare:14:16:4:psX0 votes:3:psE largest:0:8:psV sums:H:0:8 sums:Z:0:8 by_k:N:s:0:8 count:0:8:Ha count:0:8:Za
+sizes:0:8:psV dumps0 weights:1 masks:0:8:ps2 masks:0:8:ps3 places:0:8:ps3 prefix:12:16
+run0:8:16:psE run1:8:16:psE ksum lists:8:16 kblocks by_k:N:s:8:16 by_k:H:v:8:16 values:8:16
+adds:psL adds:ps2 adds:ps3 by_k:Z:s:8:16 masks:8:16:ps2:1 masks:8:16:ps3
+sums:H:8:16 sizes:8:16 count:8:16:Hb places:8:16:ps3:1 listed:0:16 sums:Z:8:16 first flags count:8:16:Zb
+lanes:H pack send second lanes:Z OW dumps1 VI UJ VB G listedO VL SU own OL keep take
 """
-LATE = {"rT": " first", "rb": " second", "dumped": " UJ", "OL": " SU"}
 
 SCRATCH = {}
 
@@ -37,15 +33,15 @@ def _declare(where, dtype, **shapes):
         SCRATCH[name] = (where, [128] + (n if isinstance(n, list) else [n]), dtype)
 
 
-_declare("sbuf", "bfloat16", B=NB + SLOTS, P=NB, PM=OFF + NB, WN=[16, 256], Y2=528, F2=528, D=256, HZ=256, NN=256, CH=256,
-         J=[4, 256], Fb=256, ob=256, m16=256, m4k=256, cE=256, c2=256, c3=256, RS=RSW, ID=128, NI=128, B1=128, BO=128, BA=128,
-         WB=128, c28=128, Ma=128, MI=128, M3=128, LE=128, LF=128, DS=128, EV=144, E1=144, WE=144, QT=16, NT=16, HT=16, iL=16,
-         wb=1, wq=1, zb=4, fo=SLOTS, PK0=128, PK1=128, PK2=128, RX0=LEAD + 128, RX1=LEAD + 128, RX2=LEAD + 128)
-_declare("sbuf", "float16", Sh=256, L2=128)
-_declare("sbuf", "float32", st=[2, 256], C0=256, C1=272, acc=4, acca=4, accb=4, accc=4, accd=4, an=4, ks=16, kc=16, zu=256,
-         m1=256, yof=256, c16=128, LS=128, I16=128, dm=4, bs=4, rc=1, r16=1, r8=1, rh=1, rn=1, rd=1, lo=1, hi=1, wm=1, wf=1)
-_declare("sbuf", "int32", SI=256, UI=256, UJ=256, VI=16, VB=16, ri=4, rb=4, rx=4, pI=1, rI=1)
-_declare("sbuf", "uint16", SU=256, kl=[2, 16], ml=4, OL=4, VL=16)
+_declare("sbuf", "bfloat16", B=NB + SLOTS, P=NB, PM=OFF + NB, WN=[16, 256], Y2=528, D=256, HF=256, ZF=256, NF=256, HC=256,
+         ZC=256, J=[4, 256], Fb=256, ob=256, m16=256, m4k=256, cE=256, c2=256, c3=256, RS=RSW, ID=128, NI=128, B1=128, BO=128,
+         BA=128, WB=128, c28=128, Ma=128, MI=128, M3=128, LE=128, LF=128, EV=144, E1=144, WE=144, QT=SLOTS, NT=16, HT=16,
+         ZT=16, iL=16, wb=1, wq=1, OW=SLOTS, fo=SLOTS, PK0=64, PK1=64, PK2=64, RX0=64, RX1=64, RX2=64)
+_declare("sbuf", "float16", Sh=256, L2=128, E0=144, G=SLOTS)
+_declare("sbuf", "float32", st=[2, 256], C0=256, C1=272, Ha=2, Hb=2, Za=2, Zb=2, ks=16, kc=16,
+         zu=256, m1=256, yof=256, c16=128, LS=128, na=2, nb=2, nd=2, bs=2, rc=1, r16=1, wm=1, wf=1)
+_declare("sbuf", "int32", SI=256, UI=256, UJ=528, VI=16, VB=16, pI=1, rI=1)
+_declare("sbuf", "uint16", SU=256, kl=[2, 16], HL=2, ZL=2, OL=2, VL=16)
 _declare("psum", "float32", psX0=512, psX1=512, psV=512, psE=512, ps2=512, ps3=512, psL=512, psO=512)
 
 DMAS = ["in_stk", "in_wt", "in_ball", "out_yo", "out_yb"]
@@ -175,8 +171,8 @@ def rank_program(g, core, T, topo):
     dma("y", "in_wt", T.wb[:], T.wt[:], [], ["wb"])
 
     balls, spare = T.B[:, 0:NB], T.B[:, 0:NB + SLOTS]
-    ps2, ps3, psE, psL = T.ps2[:, 0:256], T.ps3[:, 0:256], T.psE[:, 0:256], T.psL[:, 0:256]
-    psO, psN = T.psO[:, 0:SLOTS], T.psX0[:, 0:4]
+    ps2, ps3, psE, psL, psO = T.ps2[:, 0:256], T.ps3[:, 0:256], T.psE[:, 0:256], T.psL[:, 0:16], T.psO[:, 0:2]
+    UJ = T.UJ[:, 0:512:2]
     blk, half = [[-16, 8], [0, 16]], slice(0, 128)
 
     def factors():
@@ -190,7 +186,7 @@ def rank_program(g, core, T, topo):
     iota(T.pI[:], [[0, 1]], 0, 1, ["pI"])
     asel(T.LE[:], T.ob[:, half], blk, OP.is_equal, 0.0, 0, 1, ["ob"], ["LE"])
     asel(T.ID[:], T.ob[:, half], [[-1, 128]], OP.is_equal, 0.0, 0, 1, ["ob"], ["ID"])
-    iota(T.QT[:], [[1, 16]], 0, 0, ["QT"], **small)
+    iota(T.QT[:], [[1, SLOTS]], 0, 0, ["QT"], **small)
     asel(T.B1[:], T.ob[:, half], blk, OP.is_ge, 0.0, 0, 1, ["ob"], ["B1"])
     iota(T.C1[:], [[256, 17], [1, 16]], BASE + OFF - 1, 0, ["C1"], **small)
     asel(T.BO[:], T.B1[:], [[16, 8], [0, 16]], OP.is_ge, 0.0, 15, -1, ["B1"], ["BO"])
@@ -207,49 +203,41 @@ def rank_program(g, core, T, topo):
     ms(T.EV[:], 0.0, ["EV"])
     cp(T.rc[:], T.rI[:], ["rI"], ["rc"])
     ms(T.RS[:, 1:RSW:16], 0.0, ["RS"])
+    ms(T.UJ[:], 0, ["UJ"])
     ts(T.L2[:], T.LE[:], 2.0, None, OP.mult, None, ["LE"], ["L2"])
     cp(T.SU[:], T.SI[:], ["SI"], ["SU"])
-    ts(T.UJ[:], T.SI[:], 16.0, None, OP.mult, None, ["SI"], ["UJ"])
+    ts(UJ, T.SI[:], 16.0, None, OP.mult, None, ["SI"], ["UJ"])
     factors()
-    ts(T.hi[:], T.rc[:], 8.0, 512.0, OP.is_ge, OP.mult, ["rc"], ["hi"])
-    ts(T.lo[:], T.rc[:], 8.0, None, OP.is_lt, None, ["rc"], ["lo"])
+    ms(T.WN[:, :, 0:256:16], 0.0, ["WN"])
     ms(T.Y2[:], 0.0, ["Y2"])
-    ms(T.F2[:], 0.0, ["F2"])
     ms(T.E1[:], 0.0, ["E1"])
     ms(T.B[:, NB:NB + SLOTS], 0.0, [("B", NB, NB + SLOTS)])
     ms(T.PM[:, 0:OFF], 255.0, [("PM", 0, OFF)])
-    ms(T.F2[:, 512:528], 1.0, ["F2"])
     ms(T.kc[:], -BASE - 16.0, ["kc"])
-    ts(T.HT[:], T.QT[:], 10.0, T.lo[:], OP.is_ge, OP.mult, ["QT", "lo"], ["HT"])
-    ts(T.NT[:], T.QT[:], T.rc[:], None, OP.is_le, None, ["QT", "rc"], ["NT"])
-    ts(T.rh[:], T.rc[:], 0.5, None, OP.add, None, ["rc"], ["rh"])
-    ts(T.HT[:, 0:1], T.rc[:], 8.0, None, OP.is_ge, None, ["rc"], ["HT"])
-    ts(T.rn[:], T.rc[:], 16.0, 16.0 * NB, OP.mult, OP.add, ["rc"], ["rn"])
-    for t in range(ROUNDS):
-        ms(T["RX%d" % t][:, 0:LEAD], 0.0, [("RX%d" % t, 0, LEAD)])
-    ts(T.EV[:, 15:143:16], T.BO[:, 0:128:16], float(VOTE), None, OP.mult, None, ["BO"], ["EV"])
-    cp(T.E1[:, 15:143:16], T.BO[:, 0:128:16], ["BO"], ["E1"])
+    ts(T.HT[:], T.QT[:, 0:16], 10.0, None, OP.is_ge, None, ["QT"], ["HT"])
+    ts(T.ZT[:], T.QT[:, 0:16], 0.0, None, OP.is_equal, None, ["QT"], ["ZT"])
+    ts(T.NT[:], T.QT[:, 0:16], T.rc[:], None, OP.is_le, None, ["QT", "rc"], ["NT"])
+    for c in range(2):
+        ts(T.bs[:, c:c + 1], T.rc[:], 16.0 * c + 0.5, None, OP.add, None, ["rc"], [("bs", c, c + 1)])
+        ts(T.nb[:, c:c + 1], T.rc[:], 16.0 * c + NB - 256.0 * 4096, None, OP.add, None, ["rc"], [("nb", c, c + 1)])
     ms(T.m16[:], -16.0, ["m16"])
     ms(T.m4k[:], -4096.0, ["m4k"])
+    ts(T.EV[:, 15:143:16], T.BO[:, 0:128:16], float(VOTE), None, OP.mult, None, ["BO"], ["EV"])
+    cp(T.E1[:, 15:143:16], T.BO[:, 0:128:16], ["BO"], ["E1"])
+    ts(T.E0[:], T.E1[:], T.rc[:], None, OP.is_gt, None, ["E1", "rc"], ["E0"])
     lin("r16", "rc", 16.0)
     lin("MI", "ID", -2.0 ** 24)
     lin("NI", "ID", -1.0)
     lin("C1", "C1", 1.0, "r16")
-    lin("iL", "QT", 256.0, "r16")
+    lin("iL", "QT", 256.0, "r16", cut=slice(0, 16))
     act(T.C1[:, 0:272:16], T.C1[:, 0:272:16], AF.Identity, ["C1"], ["C1"], bias=-240.0)
-    lin("r8", "hi", -1.0 / 64, "rh")
-    lin("rd", "hi", -65536.0, "rn")
     act(T.C1[:, 1:272:16], T.ob[:, 0:17], AF.Copy, ["ob"], ["C1"], scale=float(BASE))
-    lin("DS", "ID", "hi")
-    lin("bs", "QT", 8.0, "r8", cut=slice(0, 4))
-    lin("dm", "QT", 256.0, "rd", cut=slice(0, 4))
     asel(T.LS[:], T.c16[:], [[-1, 128]], OP.is_equal, 0.0, -1, 1, ["c16"], ["LS"])
     iota(T.c3[0:1, :], [[16, 256]], 0, 0, ["c3"], **small)
     iota(T.C0[:], [[0, 16], [1, 16]], BASE - 1, 0, ["C0"], **small)
     asel(T.Ma[:], T.c28[:], [[-1, 128]], OP.is_equal, 0.0, 0, 1, ["c28"], ["Ma"])
     iota(T.C0[:, 0:256:16], [[0, 16]], BASE + 15, 0, ["C0"], **small)
     asel(T.M3[:], T.Ma[:], [[1, 128]], OP.not_equal, -2.0 ** 28, -1, -1, ["Ma"], ["M3"])
-    asel(T.I16[:], T.c16[:], [[-1, 128]], OP.is_equal, 0.0, 0, 1, ["c16"], ["I16"])
     asel(T.M3[:, 0:128:16], T.M3[:, 0:128:16], [[-16, 8]], OP.not_equal, 0.0, 1, 1, ["M3"], ["M3"])
 
     def weights(part):
@@ -286,6 +274,12 @@ def rank_program(g, core, T, topo):
                 tt(T.WN[:, j:e, d:256:s], T.P[:, 256 * j + d:256 * e:s], T[b][:, 0:16 * (e - j) * rep],
                    OP.is_lt, [("P", 256 * j, 256 * e), b], [("WN", 256 * j, 256 * e)], waw=False)
 
+        def halves(j, e, b, first=0, end=4):
+            for i in range(first, end):
+                d, s = 1 << i, 2 << i
+                tt(T.WN[:, j:e, d:256:s], T.P[:, 256 * j + d:256 * e:s], T[b][:, 0:128 * (e - j):d],
+                   OP.is_lt, [("P", 256 * j, 256 * e), b], [("WN", 256 * j, 256 * e)], waw=False)
+
         def votes(c, b, first=0, end=16):
             for q in range(first, end):
                 mm(T[b][:, 64 * c:64 * c + 64], T.EV[:, 15 - q:143 - q], T.WN[:, 4 * c:4 * c + 4, 16 * q:16 * q + 16],
@@ -304,9 +298,13 @@ def rank_program(g, core, T, topo):
             ts(T.kl[:, :, j:e], T.st[:, :, 16 * j + 1:16 * e:16], -float(BASE), None, OP.add, None,
                [("st", 16 * j, 16 * e), ("st", 256 + 16 * j, 256 + 16 * e)], [("kl", j, e), ("kl", 16 + j, 16 + e)])
 
-        def by_k(j, e, a):
-            act(T.NN[:, 16 * j:16 * e], T.NT[:, 0:16].indirect(T.kl[:, 0, j:e]), AF.Copy, ["NT", ("kl", j, e)],
-                [("NN", 16 * j, 16 * e), ("an", a, a + 1)], accum_out=T.an[:, a:a + 1])
+        def by_k(x, q, j, e):
+            out, src = T[x + "F"][:, 16 * j:16 * e], T[x + "T"][:, 0:16].indirect(T.kl[:, 0, j:e])
+            R, W = [x + "T", ("kl", j, e)], [(x + "F", 16 * j, 16 * e)]
+            if q == "s":
+                act(out, src, AF.Copy, R, W)
+            else:
+                cp(out, src, R, W)
 
         def values(j, e):
             tt(T.D[:, 16 * j:16 * e], T.PM[:, 0:OFF + 256 * e].indirect(T.kl[:, 1, j:e]), T.P[:, 256 * j:256 * e:16],
@@ -328,56 +326,57 @@ def rank_program(g, core, T, topo):
 
         def listed_o():
             for q in range(16):
-                mm(T.psO[:, 0:4], T.WE[:, 15 - q:143 - q], T[PK][:, q:SLOTS:16], False, q == 15, ["WE", (PK, 0, SLOTS)], ["psO"])
+                mm(psO, T.E0[:, 15 - q:143 - q], T.G[:, q:SLOTS:16], q == 0, q == 15, ["E0", "G"], ["psO"])
 
         def masks(j, e, b, stop=0):
             a, e, by = 16 * j, 16 * e, {"ps2": "MI", "ps3": "M3"}[b]
-            mm(T[b][:, a:e], T[by][:], T.NN[:, a:e], False, bool(stop), [by, ("NN", a, e)], [b])
+            mm(T[b][:, a:e], T[by][:], T.NF[:, a:e], False, bool(stop), [by, ("NF", a, e)], [b])
 
         def places(j, e, b, stop=0):
             mm(T[b][:, 16 * j:16 * e], T.WB[:], T.Y2[:, 32 * j:32 * e:2], False, bool(stop), ["WB", ("Y2", 32 * j, 32 * e)], [b])
 
-        def marks(j, e):
-            act(T.HZ[:, 16 * j:16 * e], T.HT[:, 0:16].indirect(T.kl[:, 0, j:e]), AF.Copy, ["HT", ("kl", j, e)],
-                [("HZ", 16 * j, 16 * e)])
+        def sums(x, j, e):
+            a, e, out, src = 16 * j, 16 * e, x + "C", x + "F"
+            scan(T[out][:, a:e], T.ob[:, a:e], T[src][:, a:e], OP.mult, OP.add,
+                 ["ob", (src, a, e)] + ([(out, a - 1, a)] if a else []), [(out, a, e)], ini=T[out][:, a - 1:a] if a else 0.0)
 
-        def sums(j, e):
-            a, e = 16 * j, 16 * e
-            scan(T.CH[:, a:e], T.ob[:, a:e], T.HZ[:, a:e], OP.mult, OP.add,
-                 ["ob", ("HZ", a, e)] + ([("CH", a - 1, a)] if a else []), [("CH", a, e)], ini=T.CH[:, a - 1:a] if a else 0.0)
+        def adds(b):
+            out, by = {"ps2": (ps2, T.m16[:]), "ps3": (ps3, T.m4k[:]), "psL": (psL, T.m4k[:, 0:16])}[b]
+            mm(out, T.BA[:], by, False, False, ["BA", "m16", "m4k"], [b])
 
-        def adds(ba, b, stop):
-            out, by = {"ps2": (ps2, T.m16[:]), "ps3": (ps3, T.m4k[:]), "psL": (T.psL[:, 0:16], T.m4k[:, 0:16]),
-                       "psO": (T.psO[:, 0:4], T.m4k[:, 0:4])}[b]
-            mm(out, T[ba][:], by, b == "psO" and ba == "BA", bool(stop), [ba, "m16", "m4k"], [b])
-
-        def count(j, e, acc, first=0, end=4):
-            a, e = 16 * j, 16 * e
-            for c in range(first, end):
-                act(T.J[:, c, a:e], T.CH[:, a:e], AF.Sign, [("CH", a, e), "bs"], [("J", 256 * c + a, 256 * c + e), (acc, c, c + 1)],
+        def count(j, e, acc):
+            a, e, src = 16 * j, 16 * e, acc[0] + "C"
+            for c in range(2):
+                r = c + 2 * (src == "ZC")
+                act(T.J[:, r, a:e], T[src][:, a:e], AF.Sign, [(src, a, e), "bs"], [("J", 256 * r + a, 256 * r + e), (acc, c, c + 1)],
                     bias=T.bs[:, c:c + 1], scale=-1.0, accum_out=T[acc][:, c:c + 1])
 
-        def pick(out, a, e, b):
-            scan(T[out][:, a:e], T.RD[:, a:e], T[b][:, a:e], OP.add, OP.max, ["RD", b], [(out, a, e)])
+        def lanes(x):
+            a, b, out = x + "a", x + "b", x + "L"
+            for c in range(2):
+                ts(T[out][:, c:c + 1], T[b][:, c:c + 1], T[a][:, c:c + 1], 256.0, OP.add, OP.add, [a, b], [(out, c, c + 1)])
 
-        def begin_list(j, e, b):
-            a, e = 16 * j, 16 * e
-            mm(T[b][:, a:e], T.MI[:], T.MO[:, a:e], True, False, ["MI", "MO"], [b])
-            mm(T[b][:, a:e], T.ob[0:1, 0:128], T.c3[0:1, a:e], False, False, ["ob", "c3"], [b])
+        def dumps(out, src, by, f):
+            for c in range(2):
+                act(T[out][:, c:c + 1], T[src][:, c:c + 1], f, [src, by], [(out, c, c + 1)], scale=4096.0, bias=T[by][:, c:c + 1])
+
+        def targets():
+            for c in range(2):
+                ts(T.OL[:, c:c + 1], T.psO[:, c:c + 1], 2048.0, T.nd[:, c:c + 1], OP.add, OP.max, ["psO", "nd"], [("OL", c, c + 1)])
 
         def pass_on():
-            send(dst, T[PK][:], T[RX][:, LEAD:LEAD + 128], [PK], "arr%d" % t)
-            landed(frm, "arr%d" % t, (RX, LEAD, LEAD + 128))
+            send(dst, T[PK][:], T[RX][:], [PK], "arr%d" % t)
+            landed(frm, "arr%d" % t, reg(RX))
 
         def stacks():
             if last:
-                ts(T.yof[:], T.UJ[:], 0.0625, None, OP.mult, None, ["UJ"], ["yof"])
+                ts(T.yof[:], UJ, 0.0625, None, OP.mult, None, ["UJ"], ["yof"])
                 dma("s", "out_yo", T.yo[:], T.yof[:], ["yof"], [])
             else:
-                ts(T.SU[:], T.UJ[:], 0.0625, None, OP.mult, None, ["UJ"], ["SU"])
+                ts(T.SU[:], UJ, 0.0625, None, OP.mult, None, ["UJ"], ["SU"])
 
         def take():
-            tt(spare.indirect(T.OL[:, 0:4]), T.fo[:], T[RX][:, 0:SLOTS], OP.add, ["OL", "fo", RX], ["B"])
+            tt(spare.indirect(T.OL[:, 0:2]), T.fo[:], T[RX][:, 0:SLOTS], OP.add, ["OL", "fo", RX], ["B"])
             if last:
                 dma("y", "out_yb", T.yb[:], balls, [("B", 0, NB)], [])
 
@@ -386,68 +385,39 @@ def rank_program(g, core, T, topo):
 
         steps = {
             "gather": gather, "tops": tops, "compare": compare, "votes": votes, "prefix": prefix, "lists": lists, "by_k": by_k,
-            "values": values, "sizes": sizes, "masks": masks, "places": places, "marks": marks, "sums": sums, "count": count,
-            "beginL": begin_list, "send": pass_on, "SU": stacks,
+            "values": values, "sizes": sizes, "masks": masks, "places": places, "sums": sums, "count": count,
+            "send": pass_on, "SU": stacks, "halves": halves,
+            "begun": lambda: None if t == 0 else factors(),
             "factors": lambda: None if last else factors(),
-            "products": lambda: tt(T.zu[:], T.UJ[:], psE, OP.mult, ["UJ", "psE"], ["zu"]),
+            "products": lambda: tt(T.zu[:], UJ, psE, OP.mult, ["UJ", "psE"], ["zu"]),
             "begin2": lambda: mm(ps2, T.ob[0:1, 0:128], T.c2[0:1, :], True, False, ["ob", "c2"], ["ps2"]),
             "begin3": lambda: mm(ps3, T.ob[0:3, 0:128], T.c3[0:3, :], True, False, ["ob", "c3"], ["ps3"]),
-            "beginO": lambda: mm(psO, T.MI[:], T.MO[:, 0:SLOTS], True, False, ["MI", "MO"], ["psO"]),
-            "beginN": lambda: mm(psN, T.I16[:], T.dm[:], True, False, ["I16", "dm"], ["psX0"]),
             "shift": lambda: mm(ps2, T.LS[:], T.zu[:], False, False, ["LS", "zu"], ["ps2"]),
             "run0": lambda j, e, b: run(0, "C0", BASE + 15.0, j, e, b),
             "run1": lambda j, e, b: run(1, "C1", T.C1[:, 16 * e:16 * e + 1], j, e, b),
-            "both": lambda: act(T.an[:, 2:3], T.an[:, 0:1], AF.Identity, [("an", 0, 2)], [("an", 2, 3)], bias=T.an[:, 1:2]),
-            "blocks": lambda ba, a: act(T[ba][:], T.BO[:], AF.Copy, ["BO", ("an", a, a + 1)], [ba], scale=T.an[:, a:a + 1]),
             "adds": adds, "weights": lambda part: None if t else weights(part),
             "ksum": lambda: scan(T.ks[:], T.kc[:], T.st[:, 0, 1:256:16], OP.add, OP.add, ["kc", ("st", 0, 256)], ["ks"]),
             "kblocks": lambda: ts(T.BA[:], T.BO[:], T.ks[:, 15:16], -1.0, OP.mult, OP.mult, ["BO", "ks"], ["BA"]),
-            "under": lambda j, e, c: ts(T.J[:, c, 16 * j:16 * e], T.CH[:, 16 * j:16 * e], T.bs[:, c:c + 1], 2.0, OP.is_lt, OP.mult,
-                                        [("CH", 16 * j, 16 * e), "bs"], [("J", 256 * c + 16 * j, 256 * c + 16 * e)]),
-            "many": lambda j, e, c, acc: do("v", lambda v: v.tensor_reduce(T[acc][:, c:c + 1], T.J[:, c, 16 * j:16 * e], AxisListType.X, OP.add),
-                                            [reg(("J", 256 * c + 16 * j, 256 * c + 16 * e))], [(acc, c, c + 1)]),
-            "less": lambda acc, c, n: act(T[acc][:, c:4], T[acc][:, c:4], AF.Identity, [acc], [acc], bias=-float(n)),
-            "addL": lambda j, e, b: mm(T[b][:, 16 * j:16 * e], T.BA[:], T.m4k[:, 16 * j:16 * e], False, True, ["BA", "m4k"], [b]),
-            "largest": largest, "listed": listed, "listedO": listed_o,
-            "beginT": lambda j, e: mm(T.psL[:, j:e], T.ID[:], T.iL[:, j:e], True, False, ["ID", "iL"], ["psL"]),
-            "addT": lambda j, e: mm(T.psL[:, j:e], T.BA[:], T.m4k[:, j:e], False, True, ["BA", "m4k"], ["psL"]),
-            "VT": lambda j, e: cp(T.VI[:, j:e], T.psL[:, j:e], ["psL"], [("VI", j, e)]),
-            "beginOT": lambda: mm(T.psO[:, 0:4], T.BA[:], T.m4k[:, 0:4], True, False, ["BA", "m4k"], ["psO"]),
-            "addOT": lambda: mm(T.psO[:, 0:4], T.ID[:], T.zb[:], False, False, ["ID", "zb"], ["psO"]),
-            "rT": lambda: cp(T.ri[:], T.psO[:, 0:4], ["psO"], ["ri"]),
-            "marked4": lambda: [ts(T.ml[:, c:c + 1], T.accb[:, c:c + 1], T.acca[:, c:c + 1], 256.0, OP.add, OP.add,
-                                   ["acca", "accb"], [("ml", c, c + 1)]) for c in range(4)],
-            "add2": lambda: mm(ps2, T.BA[:], T.m16[:], False, True, ["BA", "m16"], ["ps2"]),
-            "add3": lambda: mm(ps3, T.BA[:], T.m4k[:], False, True, ["BA", "m4k"], ["ps3"]),
-            "addO": lambda: mm(psO, T.BA[:], T.m4k[:, 0:SLOTS], False, False, ["BA", "m4k"], ["psO"]),
-            "addN": lambda: mm(psN, T.DS[:], T.zb[:], False, True, ["DS", "zb"], ["psX0"]),
-            "placesO": lambda: mm(psO, T.WB[:], T[PK][:, 0:SLOTS], False, True, ["WB", (PK, 0, SLOTS)], ["psO"]),
-            "pick": lambda j, e, b: pick("dg", 16 * j, 16 * e, b),
-            "pickO": lambda: pick("do", 0, SLOTS, "psO"),
-            "VI": lambda j, e: cp(T.VI[:, j:e], T.dg[:, 16 * j + 15:16 * e:16], [("dg", 16 * j, 16 * e)], [("VI", j, e)]),
+            "largest": largest, "listed": listed, "listedO": listed_o, "lanes": lanes, "OL": targets,
+            "beginL": lambda: mm(psL, T.ID[:], T.iL[:], True, False, ["ID", "iL"], ["psL"]),
+            "VI": lambda: cp(T.VI[:], psL, ["psL"], ["VI"]),
+            "G": lambda: ts(T.G[:], T.UJ[:, 0:528].indirect(T.ZL[:, 0:2]), 0.0625, -2048.0, OP.mult, OP.add, ["UJ", "ZL"], ["G"]),
+            "dumps0": lambda: dumps("na", "Za", "nb", AF.Identity), "dumps1": lambda: dumps("nd", "Zb", "na", AF.Relu),
             "VB": lambda: place("VB", "VI"),
             "VL": lambda: cp(T.VL[:], T.VB[:], ["VB"], ["VL"]),
             "own": lambda: cp(spare.indirect(T.VL[:, 0:16]), T.Y2[:, 0:512:2], ["VL", "Y2"], ["B"]),
-            "first": lambda: tt(T.m1[:], ps2, T.UJ[:], OP.max, ["ps2", "UJ"], ["m1"]),
+            "first": lambda: tt(T.m1[:], ps2, UJ, OP.max, ["ps2", "UJ"], ["m1"]),
             "second": lambda: tt(T.UI[:], ps3, T.m1[:], OP.max, ["ps3", "m1"], ["UI"]),
-            "UJ": lambda: ts(T.UJ[:], T.UI[:], 0xFFF0, None, OP.bitwise_and, None, ["UI"], ["UJ"]),
+            "UJ": lambda: ts(UJ, T.UI[:], 0xFFF0, None, OP.bitwise_and, None, ["UI"], ["UJ"]),
             "summed": lambda o, a, b: tt(T[o][:], T[a][:], T[b][:], OP.add, [a, b], [o]),
-            "marked": lambda: ts(T.ml[:], T.acc[:], 256.0, None, OP.add, None, ["acc"], ["ml"]),
-            "pack": lambda: act(T[PK][:, 0:SLOTS], T.Y2[:, 0:528].indirect(T.ml[:, 0:4]), AF.Copy, ["Y2", "ml"], [(PK, 0, SLOTS)]),
-            "flags": lambda: act(T[PK][:, SLOTS:128], T.F2[:, 0:528].indirect(T.ml[:, 0:4]), AF.Copy, ["F2", "ml"],
-                                 [(PK, SLOTS, 128)]),
-            "zb": lambda: lin("zb", "acc", 8.0, 2048.0),
-            "ri": lambda: tt(T.ri[:], T.do[:, 15:SLOTS:16], T.zb[:], OP.add, ["do", "zb"], ["ri"]),
-            "rb": lambda: place("rb", "ri"),
-            "dumped": lambda: tt(T.rx[:], psN, T.rb[:], OP.max, ["psX0", "rb"], ["rx"]),
-            "OL": lambda: cp(T.OL[:], T.rx[:], ["rx"], ["OL"]),
-            "keep": lambda: tt(T.fo[:], T[RX][:, SLOTS:128], T[PK][:, 0:SLOTS], OP.mult, [RX, (PK, 0, SLOTS)], ["fo"]),
+            "pack": lambda: act(T[PK][:, 0:SLOTS], T.Y2[:, 0:528].indirect(T.HL[:, 0:2]), AF.Copy, ["Y2", "HL"], [(PK, 0, SLOTS)]),
+            "OW": lambda: act(T.OW[:], T.Y2[:, 0:528].indirect(T.ZL[:, 0:2]), AF.Copy, ["Y2", "ZL"], ["OW"]),
+            "flags": lambda: ts(T[PK][:, SLOTS:64], T.QT[:], T.HC[:, 255:256], None, OP.is_ge, None, ["QT", ("HC", 255, 256)],
+                                [(PK, SLOTS, 64)]),
+            "keep": lambda: tt(T.fo[:], T[RX][:, SLOTS:64], T.OW[:], OP.mult, [RX, "OW"], ["fo"]),
             "take": take,
         }
-        words = ORDER.split()
-        if last:
-            words = " ".join(w + LATE.get(w, "") for w in words if " " + w not in LATE.values()).split()
-        for word in words:
+        for word in ORDER.split():
             name, *args = word.split(":")
             steps[name](*[int(a) if a.isdigit() else a for a in args])
 

@@ -9,21 +9,23 @@ SLOTS = 32
 VOTE = 8192
 BASE = 8 * VOTE
 OFF = 16
-RSW = 1024
+CW = 1024
 
 ORDER = """
-begun gather:s:0:2 gather:v:2:4 gather:s:4:8 gather:s:8:12 gather:s:12:14 gather:s:14:16 weights:0
-begin2 products tops:0:4:8:psX0 prefix:0:4 shift halves:0:4:psX0
-tops:4:8:8:psX1 prefix:4:8 votes:0:psV halves:4:8:psX1 begin3 beginL
-tops:8:12:8:psX0 prefix:8:12 votes:1:psV halves:8:12:psX0:0:1 run0:0:8:psV run1:0:8:psV tops:12:14:4:psX1
-halves:8:12:psX0:1:4 lists:0:8 by_k:H:s:0:8 by_k:Z:s:0:8 tops:14:16:4:psX0 votes:2:psE compare:12:14:4:psX1
-compare:14:16:4:psX0 votes:3:psE largest:0:8:psV sums:H:0:8 sums:Z:0:8 by_k:N:s:0:8 count:0:8:Ha count:0:8:Za
-sizes:0:8:psV dumps0 weights:1 masks:0:8:ps2 masks:0:8:ps3 places:0:8:ps3 prefix:12:16
-run0:8:16:psE run1:8:16:psE ksum lists:8:16 kblocks by_k:N:s:8:16 by_k:H:v:8:16 values:8:16
-adds:psL adds:ps2 adds:ps3 by_k:Z:s:8:16 masks:8:16:ps2:1 masks:8:16:ps3
-sums:H:8:16 sizes:8:16 count:8:16:Hb places:8:16:ps3:1 listed:0:16 sums:Z:8:16 first flags count:8:16:Zb
-lanes:H pack send second lanes:Z OW dumps1 VI UJ VB G listedO VL SU own OL keep take
+Sh gather:s:0:32 gather:v:32:64 gather:v:128:148 WB
+gather:s:64:128 gather:s:148:192 gather:s:192:224 gather:s:224:256
+tops:0:4:8:psX0 prefix:0:4 factors:0 tops:4:8:8:psX1 begin3 halves:0:4:psX0 votes:0:psV prefix:4:8 halves:4:8:psX1
+tops:8:12:8:psX0 prefix:8:12 votes:1:psV tops:12:14:4:psX1 halves:8:12:psX0 votes:2:psE:0:6 run0:0:8:psV run1:0:8:psV
+compare:12:14:psX1 tops:14:16:4:psX0 votes:2:psE:6:16 factors:1 factors:2 lists:0:8 compare:14:16:psX0
+by_k:H:s:0:8 votes:3:psE
+products sums:H:0:8 beginL largest:0:8:psV by_k:N:s:0:8 begin2 prefix:12:16 count:0:8:Ha shift
+run0:8:16:psE run1:8:16:psE list:0:8:16 by_k:Z:s:0:8 ksum masks:0:8:ps3 list:1:8:16 sizes:0:8:psV places:0:8:ps3
+by_k:H:s:8:16 sums:Z:0:8 kblocks adds:ps3 masks:0:8:ps2 by_k:N:s:8:16 adds:ps2 values:8:16 sizes:8:16 sums:H:8:16
+count:8:16:Hb masks:8:16:ps2:1 by_k:Z:v:8:16 flags sums:Z:8:16 first masks:8:16:ps3 places:8:16:ps3:1 lanes:H second
+count:8:16:Zb pack send adds:psL listed count:0:8:Za dumps0 dumps1 VI UJ VB lanes:Z stacks VL sooner:0:64 G listedO OW
+own OL keep sooner:64:256 take
 """
+AFTER = """sums:Z:0:8 by_k:Z:v:8:16 sums:Z:8:16 count:8:16:Zb first second""".split()
 
 SCRATCH = {}
 
@@ -33,14 +35,15 @@ def _declare(where, dtype, **shapes):
         SCRATCH[name] = (where, [128] + (n if isinstance(n, list) else [n]), dtype)
 
 
-_declare("sbuf", "bfloat16", B=NB + SLOTS, P=NB, PM=OFF + NB, WN=[16, 256], Y2=528, D=256, HF=256, ZF=256, NF=256, HC=256,
-         ZC=256, J=[4, 256], Fb=256, ob=256, m16=256, m4k=256, cE=256, c2=256, c3=256, RS=RSW, ID=128, NI=128, B1=128, BO=128,
-         BA=128, WB=128, c28=128, Ma=128, MI=128, M3=128, LE=128, LF=128, EV=144, E1=144, WE=144, QT=SLOTS, NT=16, HT=16,
-         ZT=16, iL=16, wb=1, wq=1, OW=SLOTS, fo=SLOTS, PK0=64, PK1=64, PK2=64, RX0=64, RX1=64, RX2=64)
+_declare("sbuf", "bfloat16", B=NB + SLOTS, P=NB, PM=OFF + NB, WN=[16, 256], RS=CW, Y2=528, D=256, HF=256, ZF=256,
+         NF=256, HC=256, ZC=256, J=[4, 256], Fb=256, ob=256, m16=256, m4k=256, cE=256, c2=256, c3=256, ID=128,
+         NI=128, B1=128, BO=128, BA=128, WB=128, B7=8, B8=8, Ma=128, MI=128, M3=128, LE=128, LF=128, EV=144, E1=144, WE=144,
+         QT=SLOTS, MO=SLOTS, RD=SLOTS, NT=16, HT=16, ZT=16, iL=16, wr=128, wq=1, OW=SLOTS, fo=SLOTS, PK0=64, PK1=64, PK2=64,
+         RX0=64, RX1=64, RX2=64, Z=[8, 48])
 _declare("sbuf", "float16", Sh=256, L2=128, E0=144, G=SLOTS)
-_declare("sbuf", "float32", st=[2, 256], C0=256, C1=272, Ha=2, Hb=2, Za=2, Zb=2, ks=16, kc=16,
-         zu=256, m1=256, yof=256, c16=128, LS=128, na=2, nb=2, nd=2, bs=2, rc=1, r16=1, wm=1, wf=1)
-_declare("sbuf", "int32", SI=256, UI=256, UJ=528, VI=16, VB=16, pI=1, rI=1)
+_declare("sbuf", "float32", st=[2, 256], C0=256, C1=272, Ha=2, Hb=2, Za=2, Zb=2, ks=16, kc=16, zu=256, m1=256, yof=256,
+         LS=128, dg=SLOTS, q16=SLOTS, na=2, nb=2, nd=2, bs=2, rc=1, r16=1, wm=1, wf=1)
+_declare("sbuf", "int32", SI=256, UI=256, UJ=528, VI=16, VB=16, pI=1, rI=1, wI=1, wA=1)
 _declare("sbuf", "uint16", SU=256, kl=[2, 16], HL=2, ZL=2, OL=2, VL=16)
 _declare("psum", "float32", psX0=512, psX1=512, psV=512, psE=512, ps2=512, ps3=512, psL=512, psO=512)
 
@@ -166,88 +169,103 @@ def rank_program(g, core, T, topo):
 
     small = {"allow_small_or_imprecise_dtypes": True}
 
+    dma("s", "in_wt", T.wr[0:1, :], T.wt[:], [], ["wr"])
     dma("y", "in_stk", T.SI[:], T.stk[:], [], ["SI"])
     dma("s", "in_ball", T.B[:, 0:NB], T.ball[:], [], [("B", 0, NB)])
-    dma("y", "in_wt", T.wb[:], T.wt[:], [], ["wb"])
 
     balls, spare = T.B[:, 0:NB], T.B[:, 0:NB + SLOTS]
-    ps2, ps3, psE, psL, psO = T.ps2[:, 0:256], T.ps3[:, 0:256], T.psE[:, 0:256], T.psL[:, 0:16], T.psO[:, 0:2]
+    ps2, ps3, psF, psL, psO = T.ps2[:, 0:256], T.ps3[:, 0:256], T.psL[:, 256:512], T.psL[:, 0:16], T.psO[:, 0:2]
     UJ = T.UJ[:, 0:512:2]
     blk, half = [[-16, 8], [0, 16]], slice(0, 128)
 
-    def factors():
-        ts(T.Sh[:], T.SU[:], -2048.0, None, OP.add, None, ["SU"], ["Sh"])
-        ts(T.Fb[:], T.SU[:], 1.0 / 1024, 191.5 + 1.0 / 2048, OP.mult, OP.add, ["SU"], ["Fb"])
-        mm(psE, T.ob[0:2, 0:128], T.cE[0:2, :], True, False, ["ob", "cE"], ["psE"])
-        mm(psE, T.L2[:], T.Sh[:], False, False, ["L2", "Sh"], ["psE"])
-        mm(psE, T.LF[:], T.Fb[:], False, True, ["LF", "Fb"], ["psE"])
+    def offsets(a, e):
+        ts(T.SU[:, a:e], T.UJ[:, 2 * a:2 * e:2], 0.0625, None, OP.mult, None, ["UJ"], [("SU", a, e)])
 
     ms(T.ob[:], 1.0, ["ob"])
     iota(T.pI[:], [[0, 1]], 0, 1, ["pI"])
-    asel(T.LE[:], T.ob[:, half], blk, OP.is_equal, 0.0, 0, 1, ["ob"], ["LE"])
     asel(T.ID[:], T.ob[:, half], [[-1, 128]], OP.is_equal, 0.0, 0, 1, ["ob"], ["ID"])
+    asel(T.LE[:], T.ob[:, half], blk, OP.is_equal, 0.0, 0, 1, ["ob"], ["LE"])
+    asel(T.B7[:], T.ob[:, 0:8], [[-16, 8]], OP.is_ge, 0.0, 0, 1, ["ob"], ["B7"])
     iota(T.QT[:], [[1, SLOTS]], 0, 0, ["QT"], **small)
-    asel(T.B1[:], T.ob[:, half], blk, OP.is_ge, 0.0, 0, 1, ["ob"], ["B1"])
+    asel(T.B8[:], T.B7[:], [[16, 8]], OP.is_ge, 0.0, 15, -1, ["B7"], ["B8"])
     iota(T.C1[:], [[256, 17], [1, 16]], BASE + OFF - 1, 0, ["C1"], **small)
+    iota(T.C1[:, 16:272:16], [[256, 16]], BASE + OFF + 15, 0, ["C1"], **small)
+    asel(T.B1[:], T.ob[:, half], blk, OP.is_ge, 0.0, 0, 1, ["ob"], ["B1"])
     asel(T.BO[:], T.B1[:], [[16, 8], [0, 16]], OP.is_ge, 0.0, 15, -1, ["B1"], ["BO"])
-    lin("c16", "ob", 0.0625, cut=half)
-    lin("c28", "ob", 2.0 ** 28, cut=half)
-    act(T.cE[0:2, :], T.ob[0:2, :], AF.Copy, ["ob"], ["cE"])
-    act(T.c3[0:3, :], T.ob[0:3, :], AF.Copy, ["ob"], ["c3"], scale=2.0 ** 16)
-    act(T.cE[0:1, :], T.ob[0:1, :], AF.Copy, ["ob"], ["cE"], scale=4096.0 + 2048.0 * 192)
-    act(T.c3[0:2, :], T.ob[0:2, :], AF.Copy, ["ob"], ["c3"], scale=-240.0 * 2 ** 20)
-    lin("LF", "LE", -2048.0)
-    act(T.c2[0:1, :], T.ob[0:1, :], AF.Copy, ["ob"], ["c2"], scale=2.0 ** 17)
+
+    ms(T.Z[:], 0.0, ["Z"])
     ms(T.RS[:], 1.0, ["RS"])
     ts(T.rI[:], T.pI[:], 15, None, OP.bitwise_and, None, ["pI"], ["rI"])
-    ms(T.EV[:], 0.0, ["EV"])
+    cp(T.Z[:, :, 16:32], T.ID[:], ["ID"], ["Z"])
+    ms(T.RS[:, 1:CW:16], 0.0, ["RS"])
     cp(T.rc[:], T.rI[:], ["rI"], ["rc"])
-    ms(T.RS[:, 1:RSW:16], 0.0, ["RS"])
-    ms(T.UJ[:], 0, ["UJ"])
-    ts(T.L2[:], T.LE[:], 2.0, None, OP.mult, None, ["LE"], ["L2"])
-    cp(T.SU[:], T.SI[:], ["SI"], ["SU"])
-    ts(UJ, T.SI[:], 16.0, None, OP.mult, None, ["SI"], ["UJ"])
-    factors()
-    ms(T.WN[:, :, 0:256:16], 0.0, ["WN"])
-    ms(T.Y2[:], 0.0, ["Y2"])
-    ms(T.E1[:], 0.0, ["E1"])
+    ms(T.UJ[:, 512:528], 0, [("UJ", 512, 528)])
     ms(T.B[:, NB:NB + SLOTS], 0.0, [("B", NB, NB + SLOTS)])
-    ms(T.PM[:, 0:OFF], 255.0, [("PM", 0, OFF)])
-    ms(T.kc[:], -BASE - 16.0, ["kc"])
-    ts(T.HT[:], T.QT[:, 0:16], 10.0, None, OP.is_ge, None, ["QT"], ["HT"])
-    ts(T.ZT[:], T.QT[:, 0:16], 0.0, None, OP.is_equal, None, ["QT"], ["ZT"])
-    ts(T.NT[:], T.QT[:, 0:16], T.rc[:], None, OP.is_le, None, ["QT", "rc"], ["NT"])
-    for c in range(2):
-        ts(T.bs[:, c:c + 1], T.rc[:], 16.0 * c + 0.5, None, OP.add, None, ["rc"], [("bs", c, c + 1)])
-        ts(T.nb[:, c:c + 1], T.rc[:], 16.0 * c + NB - 256.0 * 4096, None, OP.add, None, ["rc"], [("nb", c, c + 1)])
+    ms(T.WN[:, :, 0:256:16], 0.0, ["WN"])
+    tt(T.Ma[:], T.ID[:], T.Z[:, :, 15:31], OP.subtract, ["ID", "Z"], ["Ma"])
     ms(T.m16[:], -16.0, ["m16"])
     ms(T.m4k[:], -4096.0, ["m4k"])
-    ts(T.EV[:, 15:143:16], T.BO[:, 0:128:16], float(VOTE), None, OP.mult, None, ["BO"], ["EV"])
-    cp(T.E1[:, 15:143:16], T.BO[:, 0:128:16], ["BO"], ["E1"])
-    ts(T.E0[:], T.E1[:], T.rc[:], None, OP.is_gt, None, ["E1", "rc"], ["E0"])
-    lin("r16", "rc", 16.0)
-    lin("MI", "ID", -2.0 ** 24)
-    lin("NI", "ID", -1.0)
-    lin("C1", "C1", 1.0, "r16")
-    lin("iL", "QT", 256.0, "r16", cut=slice(0, 16))
-    act(T.C1[:, 0:272:16], T.C1[:, 0:272:16], AF.Identity, ["C1"], ["C1"], bias=-240.0)
-    act(T.C1[:, 1:272:16], T.ob[:, 0:17], AF.Copy, ["ob"], ["C1"], scale=float(BASE))
-    asel(T.LS[:], T.c16[:], [[-1, 128]], OP.is_equal, 0.0, -1, 1, ["c16"], ["LS"])
-    iota(T.c3[0:1, :], [[16, 256]], 0, 0, ["c3"], **small)
-    iota(T.C0[:], [[0, 16], [1, 16]], BASE - 1, 0, ["C0"], **small)
-    asel(T.Ma[:], T.c28[:], [[-1, 128]], OP.is_equal, 0.0, 0, 1, ["c28"], ["Ma"])
-    iota(T.C0[:, 0:256:16], [[0, 16]], BASE + 15, 0, ["C0"], **small)
-    asel(T.M3[:], T.Ma[:], [[1, 128]], OP.not_equal, -2.0 ** 28, -1, -1, ["Ma"], ["M3"])
-    asel(T.M3[:, 0:128:16], T.M3[:, 0:128:16], [[-16, 8]], OP.not_equal, 0.0, 1, 1, ["M3"], ["M3"])
+    ts(T.L2[:], T.LE[:], 2.0, None, OP.mult, None, ["LE"], ["L2"])
+    cp(T.SU[:], T.SI[:], ["SI"], ["SU"])
+    ts(UJ, T.SI[:], 16.0, None, OP.mult, None, ["SI"], [("UJ", 0, 512)])
+    ts(T.Sh[:], T.SU[:], -2048.0, None, OP.add, None, ["SU"], ["Sh"])
+    mm(T.psX0[:, 0:1], T.wr[0:1, :], T.ob[0:1, 0:1], True, True, ["wr", "ob"], ["psX0"])
+    cp(T.wI[:], T.psX0[:, 0:1], ["psX0"], ["wI"])
+    ms(T.c3[0:3, :], 2.0 ** 16, ["c3"])
+    ts(T.wA[:], T.wI[:], 15, None, OP.bitwise_and, None, ["wI"], ["wA"])
+    ts(T.NT[:], T.QT[:, 0:16], T.rc[:], None, OP.is_le, None, ["QT", "rc"], ["NT"])
+    ms(T.c3[0:2, :], -240.0 * 2 ** 20, ["c3"])
+    ts(T.wf[:], T.wA[:], 4096.0, None, OP.mult, None, ["wA"], ["wf"])
 
-    def weights(part):
+    act(T.cE[0:2, :], T.ob[0:2, :], AF.Copy, ["ob"], ["cE"])
+    act(T.c2[0:1, :], T.ob[0:1, :], AF.Copy, ["ob"], ["c2"], scale=2.0 ** 17)
+    act(T.cE[0:1, :], T.ob[0:1, :], AF.Copy, ["ob"], ["cE"], scale=4096.0 + 2048.0 * 192)
+    lin("EV", "ob", 0.0, cut=slice(0, 144))
+    lin("E1", "ob", 0.0, cut=slice(0, 144))
+    lin("kc", "ob", -BASE - 16.0, cut=slice(0, 16))
+    act(T.PM[:, 0:OFF], T.ob[:, 0:OFF], AF.Copy, ["ob"], [("PM", 0, OFF)], scale=255.0)
+    act(T.Y2[:, 512:528], T.ob[:, 0:16], AF.Copy, ["ob"], [("Y2", 512, 528)], scale=0.0)
+    act(T.LS[:], T.Z[:, :, 17:33], AF.Copy, ["Z"], ["LS"], scale=0.0625)
+    lin("r16", "rc", 16.0)
+    lin("LF", "ID", -2048.0)
+    lin("MI", "ID", -2.0 ** 24)
+    lin("M3", "Ma", 2.0 ** 28)
+    lin("NI", "ID", -1.0)
+    for c in range(2):
+        act(T.bs[:, c:c + 1], T.rc[:], AF.Identity, ["rc"], [("bs", c, c + 1)], bias=16.0 * c + 0.5)
+        act(T.nb[:, c:c + 1], T.rc[:], AF.Identity, ["rc"], [("nb", c, c + 1)], bias=16.0 * c + NB - 256.0 * 4096)
+    act(T.E1[:, 15:143:16], T.B8[:], AF.Copy, ["B8"], ["E1"])
+    act(T.EV[:, 15:143:16], T.B8[:], AF.Copy, ["B8"], ["EV"], scale=float(VOTE))
+    lin("iL", "QT", 256.0, "r16", cut=slice(0, 16))
+    lin("C1", "C1", 1.0, "r16")
+
+    iota(T.C0[:], [[0, 16], [1, 16]], BASE - 1, 0, ["C0"], **small)
+    iota(T.c3[0:1, :], [[16, 256]], 0, 0, ["c3"], **small)
+    iota(T.C0[:, 0:256:16], [[0, 16]], BASE + 15, 0, ["C0"], **small)
+    iota(T.C1[:, 1:272:16], [[0, 17]], BASE, 0, ["C1"], **small)
+    asel(T.HT[:], T.ob[:, 0:16], [[1, 16]], OP.is_ge, 0.0, -10, 0, ["ob"], ["HT"])
+    asel(T.ZT[:], T.ob[:, 0:16], [[1, 16]], OP.is_equal, 0.0, 0, 0, ["ob"], ["ZT"])
+
+    def factors(part):
         if part == 0:
-            lin("wq", "wb", 1.0 / 16, 191.5 + 1.0 / 32)
-            lin("wm", "wq", -65536.0, 65536.0 * 192)
-            lin("wf", "wb", 4096.0, "wm")
+            mm(T.psO[:, 0:256], T.L2[:], T.Sh[:], True, True, ["L2", "Sh"], ["psO"])
+            mm(psF, T.ob[0:2, 0:128], T.cE[0:2, :], True, False, ["ob", "cE"], ["psL"])
+            mm(psF, T.L2[:], T.Sh[:], False, False, ["L2", "Sh"], ["psL"])
+        elif part == 1:
+            act(T.Fb[:], T.psO[:, 0:256], AF.Identity, ["psO"], ["Fb"], scale=1.0 / 2048, bias=193.5 + 1.0 / 2048)
         else:
-            lin("WB", "BO", "wf")
-            lin("WE", "E1", "wf")
+            mm(psF, T.LF[:], T.Fb[:], False, True, ["LF", "Fb"], ["psL"])
+
+    ahead = {
+        "factors": factors,
+        "products": lambda: tt(T.zu[:], UJ, psF, OP.mult, ["UJ", "psL"], ["zu"]),
+        "begin2": lambda: mm(ps2, T.ob[0:1, 0:128], T.c2[0:1, :], True, False, ["ob", "c2"], ["ps2"]),
+        "shift": lambda: mm(ps2, T.LS[:], T.zu[:], False, False, ["LS", "zu"], ["ps2"]),
+    }
+    for part in range(3):
+        factors(part)
+    ts(T.E0[:], T.E1[:], T.rc[:], None, OP.is_gt, None, ["E1", "rc"], ["E0"])
+    ts(T.WE[:], T.E1[:], T.wf[:], None, OP.mult, None, ["E1", "wf"], ["WE"])
 
     def throw(t):
         last = t == ROUNDS - 1
@@ -255,23 +273,23 @@ def rank_program(g, core, T, topo):
         dst, frm = T.cores[(rank + t + 1) % n], T.cores[(rank - t - 1) % n]
         PK, RX = "PK%d" % t, "RX%d" % t
 
-        def gather(q, j, e):
-            out, off = T.P[:, 256 * j:256 * e], T.SU[:, 16 * j:16 * e]
-            R, W = [("B", 0, NB), ("SU", 16 * j, 16 * e)], [("P", 256 * j, 256 * e)]
+        def by_list(q, out, src, R, W):
             if q == "s":
-                act(out, balls.indirect(off), AF.Copy, R, W)
+                act(out, src, AF.Copy, R, W)
             else:
-                cp(out, balls.indirect(off), R, W)
+                cp(out, src, R, W)
+
+        def gather(q, a, e):
+            by_list(q, T.P[:, 16 * a:16 * e], balls.indirect(T.SU[:, a:e]), [("B", 0, NB), ("SU", a, e)], [("P", 16 * a, 16 * e)])
 
         def tops(j, e, rep, b):
             for r in range(rep):
                 mm(T[b][:, r:16 * (e - j) * rep:rep], T.ID[:], T.P[:, 256 * j:256 * e:16], True, True,
                    ["ID", ("P", 256 * j, 256 * e)], [b])
 
-        def compare(j, e, rep, b, first=0, end=16):
-            s = 16 // rep
-            for d in range(first, min(end, s)):
-                tt(T.WN[:, j:e, d:256:s], T.P[:, 256 * j + d:256 * e:s], T[b][:, 0:16 * (e - j) * rep],
+        def compare(j, e, b):
+            for d in range(4):
+                tt(T.WN[:, j:e, d:256:4], T.P[:, 256 * j + d:256 * e:4], T[b][:, 0:64 * (e - j)],
                    OP.is_lt, [("P", 256 * j, 256 * e), b], [("WN", 256 * j, 256 * e)], waw=False)
 
         def halves(j, e, b, first=0, end=4):
@@ -283,7 +301,7 @@ def rank_program(g, core, T, topo):
         def votes(c, b, first=0, end=16):
             for q in range(first, end):
                 mm(T[b][:, 64 * c:64 * c + 64], T.EV[:, 15 - q:143 - q], T.WN[:, 4 * c:4 * c + 4, 16 * q:16 * q + 16],
-                   q == 0, q == 15, ["EV", ("WN", 1024 * c, 1024 * c + 1024)], [b])
+                   q == 0, q == 15, ["EV", ("WN", CW * c, CW * c + CW)], [b])
 
         def prefix(j, e):
             scan(T.PM[:, OFF + 256 * j:OFF + 256 * e], T.RS[:, 0:256 * (e - j)], T.P[:, 256 * j:256 * e], OP.mult, OP.max,
@@ -298,13 +316,13 @@ def rank_program(g, core, T, topo):
             ts(T.kl[:, :, j:e], T.st[:, :, 16 * j + 1:16 * e:16], -float(BASE), None, OP.add, None,
                [("st", 16 * j, 16 * e), ("st", 256 + 16 * j, 256 + 16 * e)], [("kl", j, e), ("kl", 16 + j, 16 + e)])
 
+        def list_one(i, j, e):
+            ts(T.kl[:, i, j:e], T.st[:, i, 16 * j + 1:16 * e:16], -float(BASE), None, OP.add, None,
+               [("st", 256 * i + 16 * j, 256 * i + 16 * e)], [("kl", 16 * i + j, 16 * i + e)])
+
         def by_k(x, q, j, e):
-            out, src = T[x + "F"][:, 16 * j:16 * e], T[x + "T"][:, 0:16].indirect(T.kl[:, 0, j:e])
-            R, W = [x + "T", ("kl", j, e)], [(x + "F", 16 * j, 16 * e)]
-            if q == "s":
-                act(out, src, AF.Copy, R, W)
-            else:
-                cp(out, src, R, W)
+            by_list(q, T[x + "F"][:, 16 * j:16 * e], T[x + "T"][:, 0:16].indirect(T.kl[:, 0, j:e]), [x + "T", ("kl", j, e)],
+                    [(x + "F", 16 * j, 16 * e)])
 
         def values(j, e):
             tt(T.D[:, 16 * j:16 * e], T.PM[:, 0:OFF + 256 * e].indirect(T.kl[:, 1, j:e]), T.P[:, 256 * j:256 * e:16],
@@ -319,10 +337,9 @@ def rank_program(g, core, T, topo):
         def sizes(j, e, b="D"):
             act(T.Y2[:, 32 * j:32 * e:2], T[b][:, 16 * j:16 * e], AF.Abs, [(b, 16 * j, 16 * e)], [("Y2", 32 * j, 32 * e)])
 
-        def listed(j, e):
+        def listed():
             for q in range(16):
-                mm(T.psL[:, j:e], T.WE[:, 15 - q:143 - q], T.Y2[:, 32 * j + 2 * q:32 * e:32], False, q == 15 and e == 16,
-                   ["WE", ("Y2", 32 * j, 32 * e)], ["psL"])
+                mm(psL, T.WE[:, 15 - q:143 - q], T.Y2[:, 2 * q:512:32], False, q == 15, ["WE", "Y2"], ["psL"])
 
         def listed_o():
             for q in range(16):
@@ -372,57 +389,55 @@ def rank_program(g, core, T, topo):
             if last:
                 ts(T.yof[:], UJ, 0.0625, None, OP.mult, None, ["UJ"], ["yof"])
                 dma("s", "out_yo", T.yo[:], T.yof[:], ["yof"], [])
-            else:
-                ts(T.SU[:], UJ, 0.0625, None, OP.mult, None, ["UJ"], ["SU"])
 
         def take():
-            tt(spare.indirect(T.OL[:, 0:2]), T.fo[:], T[RX][:, 0:SLOTS], OP.add, ["OL", "fo", RX], ["B"])
+            tt(spare.indirect(T.OL[:, 0:2]), T.fo[:], T[RX][:, 0:SLOTS], OP.add, ["OL", "fo", RX], [("B", 0, NB + SLOTS)])
             if last:
                 dma("y", "out_yb", T.yb[:], balls, [("B", 0, NB)], [])
 
-        def place(out, src):
-            ts(T[out][:], T[src][:], 4, 4095, OP.arith_shift_right, OP.bitwise_and, [src], [out])
-
         steps = {
-            "gather": gather, "tops": tops, "compare": compare, "votes": votes, "prefix": prefix, "lists": lists, "by_k": by_k,
-            "values": values, "sizes": sizes, "masks": masks, "places": places, "sums": sums, "count": count,
-            "send": pass_on, "SU": stacks, "halves": halves,
-            "begun": lambda: None if t == 0 else factors(),
-            "factors": lambda: None if last else factors(),
-            "products": lambda: tt(T.zu[:], UJ, psE, OP.mult, ["UJ", "psE"], ["zu"]),
-            "begin2": lambda: mm(ps2, T.ob[0:1, 0:128], T.c2[0:1, :], True, False, ["ob", "c2"], ["ps2"]),
+            "tops": tops, "compare": compare, "halves": halves,
+            "Sh": lambda: ts(T.Sh[:], T.SU[:], -2048.0, None, OP.add, None, ["SU"], ["Sh"]) if t else None,
+            "listedO": listed_o,
+            "WB": lambda: None if t else ts(T.WB[:], T.BO[:], T.wf[:], None, OP.mult, None, ["BO", "wf"], ["WB"]),
+            "gather": gather, "votes": votes, "prefix": prefix, "lists": lists,
+            "list": list_one, "by_k": by_k, "values": values, "largest": largest, "sizes": sizes, "listed": listed,
+            "masks": masks, "places": places, "sums": sums, "adds": adds, "count": count, "lanes": lanes, "OL": targets,
+            "send": pass_on, "stacks": stacks, "take": take,
+            "sooner": lambda a, e: None if last else offsets(a, e), "later": lambda a, e: offsets(a, e) if t else None,
             "begin3": lambda: mm(ps3, T.ob[0:3, 0:128], T.c3[0:3, :], True, False, ["ob", "c3"], ["ps3"]),
-            "shift": lambda: mm(ps2, T.LS[:], T.zu[:], False, False, ["LS", "zu"], ["ps2"]),
+            "beginL": lambda: mm(psL, T.ID[:], T.iL[:], True, False, ["ID", "iL"], ["psL"]),
             "run0": lambda j, e, b: run(0, "C0", BASE + 15.0, j, e, b),
             "run1": lambda j, e, b: run(1, "C1", T.C1[:, 16 * e:16 * e + 1], j, e, b),
-            "adds": adds, "weights": lambda part: None if t else weights(part),
             "ksum": lambda: scan(T.ks[:], T.kc[:], T.st[:, 0, 1:256:16], OP.add, OP.add, ["kc", ("st", 0, 256)], ["ks"]),
             "kblocks": lambda: ts(T.BA[:], T.BO[:], T.ks[:, 15:16], -1.0, OP.mult, OP.mult, ["BO", "ks"], ["BA"]),
-            "largest": largest, "listed": listed, "listedO": listed_o, "lanes": lanes, "OL": targets,
-            "beginL": lambda: mm(psL, T.ID[:], T.iL[:], True, False, ["ID", "iL"], ["psL"]),
             "VI": lambda: cp(T.VI[:], psL, ["psL"], ["VI"]),
-            "G": lambda: ts(T.G[:], T.UJ[:, 0:528].indirect(T.ZL[:, 0:2]), 0.0625, -2048.0, OP.mult, OP.add, ["UJ", "ZL"], ["G"]),
-            "dumps0": lambda: dumps("na", "Za", "nb", AF.Identity), "dumps1": lambda: dumps("nd", "Zb", "na", AF.Relu),
-            "VB": lambda: place("VB", "VI"),
+            "VB": lambda: ts(T.VB[:], T.VI[:], 4, 4095, OP.arith_shift_right, OP.bitwise_and, ["VI"], ["VB"]),
             "VL": lambda: cp(T.VL[:], T.VB[:], ["VB"], ["VL"]),
-            "own": lambda: cp(spare.indirect(T.VL[:, 0:16]), T.Y2[:, 0:512:2], ["VL", "Y2"], ["B"]),
+            "own": lambda: cp(spare.indirect(T.VL[:, 0:16]), T.Y2[:, 0:512:2], ["VL", "Y2"], [("B", 0, NB + SLOTS)]),
             "first": lambda: tt(T.m1[:], ps2, UJ, OP.max, ["ps2", "UJ"], ["m1"]),
             "second": lambda: tt(T.UI[:], ps3, T.m1[:], OP.max, ["ps3", "m1"], ["UI"]),
             "UJ": lambda: ts(UJ, T.UI[:], 0xFFF0, None, OP.bitwise_and, None, ["UI"], ["UJ"]),
-            "summed": lambda o, a, b: tt(T[o][:], T[a][:], T[b][:], OP.add, [a, b], [o]),
+            "G": lambda: ts(T.G[:], T.UJ[:, 0:528].indirect(T.ZL[:, 0:2]), 0.0625, -2048.0, OP.mult, OP.add, ["UJ", "ZL"], ["G"]),
+            "dumps0": lambda: dumps("na", "Za", "nb", AF.Identity), "dumps1": lambda: dumps("nd", "Zb", "na", AF.Relu),
             "pack": lambda: act(T[PK][:, 0:SLOTS], T.Y2[:, 0:528].indirect(T.HL[:, 0:2]), AF.Copy, ["Y2", "HL"], [(PK, 0, SLOTS)]),
             "OW": lambda: act(T.OW[:], T.Y2[:, 0:528].indirect(T.ZL[:, 0:2]), AF.Copy, ["Y2", "ZL"], ["OW"]),
             "flags": lambda: ts(T[PK][:, SLOTS:64], T.QT[:], T.HC[:, 255:256], None, OP.is_ge, None, ["QT", ("HC", 255, 256)],
                                 [(PK, SLOTS, 64)]),
             "keep": lambda: tt(T.fo[:], T[RX][:, SLOTS:64], T.OW[:], OP.mult, [RX, "OW"], ["fo"]),
-            "take": take,
         }
-        for word in ORDER.split():
+        steps.update(ahead)
+        words = ORDER.split()
+        if t == 0:
+            words = [w for w in words if w.split(":")[0] != "factors"]
+            cut = words.index("send") + 1
+            words = ([w for w in words[:cut] if w not in AFTER] + [w for w in words[:cut] if w in AFTER] + words[cut:])
+        for word in words:
             name, *args = word.split(":")
             steps[name](*[int(a) if a.isdigit() else a for a in args])
 
     for t in range(ROUNDS):
         throw(t)
 
-    for sem in sorted(total):
+    for sem in sorted(total, key=lambda s: s == "dma_out_yb"):
         wait_for("g", sem, total[sem], {})

import numpy as np
from concourse.mybir import AluOpType, ActivationFunctionType

OP = AluOpType
AF = ActivationFunctionType
ROUNDS = 3
NB = 4096
SLOTS = 32
VOTE = 8192
BASE = 8 * VOTE
OFF = 16
CW = 1024

ORDER = """
Sh gather:s:0:32 gather:v:32:64 gather:v:128:148 WB
gather:s:64:128 gather:s:148:192 gather:s:192:224 gather:s:224:256
tops:0:4:8:psX0 prefix:0:4 factors:0 tops:4:8:8:psX1 begin3 halves:0:4:psX0 votes:0:psV prefix:4:8 halves:4:8:psX1
tops:8:12:8:psX0 prefix:8:12 votes:1:psV tops:12:14:4:psX1 halves:8:12:psX0 votes:2:psE:0:6 run0:0:8:psV run1:0:8:psV
compare:12:14:psX1 tops:14:16:4:psX0 votes:2:psE:6:16 factors:1 factors:2 lists:0:8 compare:14:16:psX0
by_k:H:s:0:8 votes:3:psE
products sums:H:0:8 beginL largest:0:8:psV by_k:N:s:0:8 begin2 prefix:12:16 count:0:8:Ha shift
run0:8:16:psE run1:8:16:psE list:0:8:16 by_k:Z:s:0:8 ksum masks:0:8:ps3 list:1:8:16 sizes:0:8:psV places:0:8:ps3
by_k:H:s:8:16 sums:Z:0:8 kblocks adds:ps3 masks:0:8:ps2 by_k:N:s:8:16 adds:ps2 values:8:16 sizes:8:16 sums:H:8:16
count:8:16:Hb masks:8:16:ps2:1 by_k:Z:v:8:16 flags sums:Z:8:16 first masks:8:16:ps3 places:8:16:ps3:1 lanes:H second
count:8:16:Zb pack send adds:psL listed count:0:8:Za dumps0 dumps1 VI UJ VB lanes:Z stacks VL sooner:0:64 G listedO OW
own OL keep sooner:64:256 take
"""
AFTER = """sums:Z:0:8 by_k:Z:v:8:16 sums:Z:8:16 count:8:16:Zb first second""".split()

SCRATCH = {}


def _declare(where, dtype, **shapes):
    for name, n in shapes.items():
        SCRATCH[name] = (where, [128] + (n if isinstance(n, list) else [n]), dtype)


_declare("sbuf", "bfloat16", B=NB + SLOTS, P=NB, PM=OFF + NB, WN=[16, 256], RS=CW, Y2=528, D=256, HF=256, ZF=256,
         NF=256, HC=256, ZC=256, J=[4, 256], Fb=256, ob=256, m16=256, m4k=256, cE=256, c2=256, c3=256, ID=128,
         NI=128, B1=128, BO=128, BA=128, WB=128, B7=8, B8=8, Ma=128, MI=128, M3=128, LE=128, LF=128, EV=144, E1=144, WE=144,
         QT=SLOTS, MO=SLOTS, RD=SLOTS, NT=16, HT=16, ZT=16, iL=16, wr=128, wq=1, OW=SLOTS, fo=SLOTS, PK0=64, PK1=64, PK2=64,
         RX0=64, RX1=64, RX2=64, Z=[8, 48])
_declare("sbuf", "float16", Sh=256, L2=128, E0=144, G=SLOTS)
_declare("sbuf", "float32", st=[2, 256], C0=256, C1=272, Ha=2, Hb=2, Za=2, Zb=2, ks=16, kc=16, zu=256, m1=256, yof=256,
         LS=128, dg=SLOTS, q16=SLOTS, na=2, nb=2, nd=2, bs=2, rc=1, r16=1, wm=1, wf=1)
_declare("sbuf", "int32", SI=256, UI=256, UJ=528, VI=16, VB=16, pI=1, rI=1, wI=1, wA=1)
_declare("sbuf", "uint16", SU=256, kl=[2, 16], HL=2, ZL=2, OL=2, VL=16)
_declare("psum", "float32", psX0=512, psX1=512, psV=512, psE=512, ps2=512, ps3=512, psL=512, psO=512)

DMAS = ["in_stk", "in_wt", "in_ball", "out_yo", "out_yb"]
SEMAPHORES = ["qv", "qs", "qt", "qg", "ls"] + ["dma_" + d for d in DMAS] + ["arr%d" % t for t in range(ROUNDS)]


def rank_program(g, core, T, topo):
    rank = T.rank_of(core)
    if rank is None:
        return
    queues = {"g": g, "v": g.vector, "s": g.scalar, "t": g.tensor, "y": g.sync}
    qsem = {"g": "qg", "v": "qv", "s": "qs", "t": "qt"}
    total = {}
    know = dict((q, {}) for q in queues)
    hist = {}

    def wait_for(q, sem, val, clock):
        if know[q].get(sem, 0) >= val:
            return
        queues[q].wait_ge(T.sem[sem], val)
        know[q][sem] = val
        for s2, v2 in clock.items():
            if know[q].get(s2, 0) < v2:
                know[q][s2] = v2

    def need(q, reads, writes, waw=True):
        deps = []
        for acc, isw in ((reads, False), (writes, True)):
            for (b, lo, hi) in acc:
                for h in hist.get(b, ()):
                    same = h[3] == q
                    if b.startswith("ps") and not same:
                        deps.append(h)
                        continue
                    if h[1] <= lo or hi <= h[0] or not (isw or h[2]):
                        continue
                    if same and (q == "t" or (isw and (not h[2] or not waw))):
                        continue
                    deps.append(h)
        for h in sorted(deps, key=lambda h: -h[5]):
            wait_for(q, h[4], h[5], h[6])

    def note(q, sem, val, reads, writes):
        clock = dict(know.get(q, {}))
        clock[sem] = max(clock.get(sem, 0), val)
        for acc, isw in ((reads, False), (writes, True)):
            for (b, lo, hi) in acc:
                old = hist.get(b, [])
                if isw and b.startswith("ps"):
                    old = []
                elif isw:
                    old = [h for h in old if not (lo <= h[0] and h[1] <= hi)]
                else:
                    old = [h for h in old if not (h[3] == q and not h[2] and lo <= h[0] and h[1] <= hi)]
                hist[b] = old + [(lo, hi, isw, q, sem, val, clock)]

    def reg(r):
        return r if isinstance(r, tuple) else (r, 0, int(np.prod(SCRATCH[r][1][1:])))

    def do(q, call, reads, writes, waw=True):
        R, W = [reg(r) for r in reads], [reg(w) for w in writes]
        need(q, R, W, waw)
        sem = qsem[q]
        total[sem] = total.get(sem, 0) + 1
        call(queues[q]).then_inc(T.sem[sem], 1)
        note(q, sem, total[sem], R, W)

    def dma(q, name, out, in_, reads, writes):
        R, W = [reg(r) for r in reads], [reg(w) for w in writes]
        need(q, R, W)
        sem = "dma_" + name
        total[sem] = 16
        queues[q].dma_start(out, in_).then_inc(T.sem[sem], 16)
        note(sem, sem, 16, R, W)

    def lanes_of(src, dst):
        return topo.engines(src, dst)[:8]

    def send(dst, src, out, reads, sem):
        need("g", [reg(r) for r in reads], [])
        rid, pid, _ = topo.addr(dst)
        eng = lanes_of(core, dst)
        total["ls"] = total.get("ls", 0) + len(eng)
        g.remote_dma(out, src, T.sem[sem], T.sem["ls"], pid, rid, sum(1 << e for e in eng))

    def landed(frm, sem, where):
        total[sem] = len(lanes_of(frm, core))
        note("remote", sem, total[sem], [], [where])

    def ts(out, in0, s1, s2, op0, op1, R, W):
        ops = (op0,) if op1 is None else (op0, op1)
        do("v", lambda v: v.tensor_scalar(out, in0, s1, s2, *ops), R, W)

    def tt(out, a, b, op, R, W, waw=True):
        do("v", lambda v: v.tensor_tensor(out, a, b, op), R, W, waw)

    def cp(out, a, R, W):
        do("v", lambda v: v.tensor_copy(out, a), R, W)

    def ms(out, c, W):
        do("v", lambda v: v.memset(out, c), [], W)

    def scan(out, d0, d1, o0, o1, R, W, ini=0.0):
        do("v", lambda v: v.tensor_tensor_scan(out, d0, d1, ini, o0, o1), R, W)

    def act(out, a, f, R, W, **kw):
        do("s", lambda s: s.activation(out, a, f, **kw), R, W)

    def lin(out, src, scale, bias=0.0, f=AF.Identity, cut=slice(None)):
        cols = [x for x in (scale, bias) if isinstance(x, str)]
        act(T[out][:], T[src][:, cut], f, [src] + cols, [out], scale=T[scale][:] if isinstance(scale, str) else scale,
            bias=T[bias][:] if isinstance(bias, str) else bias)

    def mm(out, l, r, start, stop, R, W):
        do("t", lambda x: x.matmul(out, l, r, start, stop), R, W)

    def asel(out, a, pat, cmp, fill, base, mult, R, W):
        do("g", lambda x: x.affine_select(out, a, pat, cmp, fill, base, mult), R, W)

    def iota(out, pat, base, mult, W, **kw):
        do("g", lambda x: x.iota(out, pat, base, mult, **kw), [], W)

    small = {"allow_small_or_imprecise_dtypes": True}

    dma("s", "in_wt", T.wr[0:1, :], T.wt[:], [], ["wr"])
    dma("y", "in_stk", T.SI[:], T.stk[:], [], ["SI"])
    dma("s", "in_ball", T.B[:, 0:NB], T.ball[:], [], [("B", 0, NB)])

    balls, spare = T.B[:, 0:NB], T.B[:, 0:NB + SLOTS]
    ps2, ps3, psF, psL, psO = T.ps2[:, 0:256], T.ps3[:, 0:256], T.psL[:, 256:512], T.psL[:, 0:16], T.psO[:, 0:2]
    UJ = T.UJ[:, 0:512:2]
    blk, half = [[-16, 8], [0, 16]], slice(0, 128)

    def offsets(a, e):
        ts(T.SU[:, a:e], T.UJ[:, 2 * a:2 * e:2], 0.0625, None, OP.mult, None, ["UJ"], [("SU", a, e)])

    ms(T.ob[:], 1.0, ["ob"])
    iota(T.pI[:], [[0, 1]], 0, 1, ["pI"])
    asel(T.ID[:], T.ob[:, half], [[-1, 128]], OP.is_equal, 0.0, 0, 1, ["ob"], ["ID"])
    asel(T.LE[:], T.ob[:, half], blk, OP.is_equal, 0.0, 0, 1, ["ob"], ["LE"])
    asel(T.B7[:], T.ob[:, 0:8], [[-16, 8]], OP.is_ge, 0.0, 0, 1, ["ob"], ["B7"])
    iota(T.QT[:], [[1, SLOTS]], 0, 0, ["QT"], **small)
    asel(T.B8[:], T.B7[:], [[16, 8]], OP.is_ge, 0.0, 15, -1, ["B7"], ["B8"])
    iota(T.C1[:], [[256, 17], [1, 16]], BASE + OFF - 1, 0, ["C1"], **small)
    iota(T.C1[:, 16:272:16], [[256, 16]], BASE + OFF + 15, 0, ["C1"], **small)
    asel(T.B1[:], T.ob[:, half], blk, OP.is_ge, 0.0, 0, 1, ["ob"], ["B1"])
    asel(T.BO[:], T.B1[:], [[16, 8], [0, 16]], OP.is_ge, 0.0, 15, -1, ["B1"], ["BO"])

    ms(T.Z[:], 0.0, ["Z"])
    ms(T.RS[:], 1.0, ["RS"])
    ts(T.rI[:], T.pI[:], 15, None, OP.bitwise_and, None, ["pI"], ["rI"])
    cp(T.Z[:, :, 16:32], T.ID[:], ["ID"], ["Z"])
    ms(T.RS[:, 1:CW:16], 0.0, ["RS"])
    cp(T.rc[:], T.rI[:], ["rI"], ["rc"])
    ms(T.UJ[:, 512:528], 0, [("UJ", 512, 528)])
    ms(T.B[:, NB:NB + SLOTS], 0.0, [("B", NB, NB + SLOTS)])
    ms(T.WN[:, :, 0:256:16], 0.0, ["WN"])
    tt(T.Ma[:], T.ID[:], T.Z[:, :, 15:31], OP.subtract, ["ID", "Z"], ["Ma"])
    ms(T.m16[:], -16.0, ["m16"])
    ms(T.m4k[:], -4096.0, ["m4k"])
    ts(T.L2[:], T.LE[:], 2.0, None, OP.mult, None, ["LE"], ["L2"])
    cp(T.SU[:], T.SI[:], ["SI"], ["SU"])
    ts(UJ, T.SI[:], 16.0, None, OP.mult, None, ["SI"], [("UJ", 0, 512)])
    ts(T.Sh[:], T.SU[:], -2048.0, None, OP.add, None, ["SU"], ["Sh"])
    mm(T.psX0[:, 0:1], T.wr[0:1, :], T.ob[0:1, 0:1], True, True, ["wr", "ob"], ["psX0"])
    cp(T.wI[:], T.psX0[:, 0:1], ["psX0"], ["wI"])
    ms(T.c3[0:3, :], 2.0 ** 16, ["c3"])
    ts(T.wA[:], T.wI[:], 15, None, OP.bitwise_and, None, ["wI"], ["wA"])
    ts(T.NT[:], T.QT[:, 0:16], T.rc[:], None, OP.is_le, None, ["QT", "rc"], ["NT"])
    ms(T.c3[0:2, :], -240.0 * 2 ** 20, ["c3"])
    ts(T.wf[:], T.wA[:], 4096.0, None, OP.mult, None, ["wA"], ["wf"])

    act(T.cE[0:2, :], T.ob[0:2, :], AF.Copy, ["ob"], ["cE"])
    act(T.c2[0:1, :], T.ob[0:1, :], AF.Copy, ["ob"], ["c2"], scale=2.0 ** 17)
    act(T.cE[0:1, :], T.ob[0:1, :], AF.Copy, ["ob"], ["cE"], scale=4096.0 + 2048.0 * 192)
    lin("EV", "ob", 0.0, cut=slice(0, 144))
    lin("E1", "ob", 0.0, cut=slice(0, 144))
    lin("kc", "ob", -BASE - 16.0, cut=slice(0, 16))
    act(T.PM[:, 0:OFF], T.ob[:, 0:OFF], AF.Copy, ["ob"], [("PM", 0, OFF)], scale=255.0)
    act(T.Y2[:, 512:528], T.ob[:, 0:16], AF.Copy, ["ob"], [("Y2", 512, 528)], scale=0.0)
    act(T.LS[:], T.Z[:, :, 17:33], AF.Copy, ["Z"], ["LS"], scale=0.0625)
    lin("r16", "rc", 16.0)
    lin("LF", "ID", -2048.0)
    lin("MI", "ID", -2.0 ** 24)
    lin("M3", "Ma", 2.0 ** 28)
    lin("NI", "ID", -1.0)
    for c in range(2):
        act(T.bs[:, c:c + 1], T.rc[:], AF.Identity, ["rc"], [("bs", c, c + 1)], bias=16.0 * c + 0.5)
        act(T.nb[:, c:c + 1], T.rc[:], AF.Identity, ["rc"], [("nb", c, c + 1)], bias=16.0 * c + NB - 256.0 * 4096)
    act(T.E1[:, 15:143:16], T.B8[:], AF.Copy, ["B8"], ["E1"])
    act(T.EV[:, 15:143:16], T.B8[:], AF.Copy, ["B8"], ["EV"], scale=float(VOTE))
    lin("iL", "QT", 256.0, "r16", cut=slice(0, 16))
    lin("C1", "C1", 1.0, "r16")

    iota(T.C0[:], [[0, 16], [1, 16]], BASE - 1, 0, ["C0"], **small)
    iota(T.c3[0:1, :], [[16, 256]], 0, 0, ["c3"], **small)
    iota(T.C0[:, 0:256:16], [[0, 16]], BASE + 15, 0, ["C0"], **small)
    iota(T.C1[:, 1:272:16], [[0, 17]], BASE, 0, ["C1"], **small)
    asel(T.HT[:], T.ob[:, 0:16], [[1, 16]], OP.is_ge, 0.0, -10, 0, ["ob"], ["HT"])
    asel(T.ZT[:], T.ob[:, 0:16], [[1, 16]], OP.is_equal, 0.0, 0, 0, ["ob"], ["ZT"])

    def factors(part):
        if part == 0:
            mm(T.psO[:, 0:256], T.L2[:], T.Sh[:], True, True, ["L2", "Sh"], ["psO"])
            mm(psF, T.ob[0:2, 0:128], T.cE[0:2, :], True, False, ["ob", "cE"], ["psL"])
            mm(psF, T.L2[:], T.Sh[:], False, False, ["L2", "Sh"], ["psL"])
        elif part == 1:
            act(T.Fb[:], T.psO[:, 0:256], AF.Identity, ["psO"], ["Fb"], scale=1.0 / 2048, bias=193.5 + 1.0 / 2048)
        else:
            mm(psF, T.LF[:], T.Fb[:], False, True, ["LF", "Fb"], ["psL"])

    ahead = {
        "factors": factors,
        "products": lambda: tt(T.zu[:], UJ, psF, OP.mult, ["UJ", "psL"], ["zu"]),
        "begin2": lambda: mm(ps2, T.ob[0:1, 0:128], T.c2[0:1, :], True, False, ["ob", "c2"], ["ps2"]),
        "shift": lambda: mm(ps2, T.LS[:], T.zu[:], False, False, ["LS", "zu"], ["ps2"]),
    }
    for part in range(3):
        factors(part)
    ts(T.E0[:], T.E1[:], T.rc[:], None, OP.is_gt, None, ["E1", "rc"], ["E0"])
    ts(T.WE[:], T.E1[:], T.wf[:], None, OP.mult, None, ["E1", "wf"], ["WE"])

    def throw(t):
        last = t == ROUNDS - 1
        n = len(T.cores)
        dst, frm = T.cores[(rank + t + 1) % n], T.cores[(rank - t - 1) % n]
        PK, RX = "PK%d" % t, "RX%d" % t

        def by_list(q, out, src, R, W):
            if q == "s":
                act(out, src, AF.Copy, R, W)
            else:
                cp(out, src, R, W)

        def gather(q, a, e):
            by_list(q, T.P[:, 16 * a:16 * e], balls.indirect(T.SU[:, a:e]), [("B", 0, NB), ("SU", a, e)], [("P", 16 * a, 16 * e)])

        def tops(j, e, rep, b):
            for r in range(rep):
                mm(T[b][:, r:16 * (e - j) * rep:rep], T.ID[:], T.P[:, 256 * j:256 * e:16], True, True,
                   ["ID", ("P", 256 * j, 256 * e)], [b])

        def compare(j, e, b):
            for d in range(4):
                tt(T.WN[:, j:e, d:256:4], T.P[:, 256 * j + d:256 * e:4], T[b][:, 0:64 * (e - j)],
                   OP.is_lt, [("P", 256 * j, 256 * e), b], [("WN", 256 * j, 256 * e)], waw=False)

        def halves(j, e, b, first=0, end=4):
            for i in range(first, end):
                d, s = 1 << i, 2 << i
                tt(T.WN[:, j:e, d:256:s], T.P[:, 256 * j + d:256 * e:s], T[b][:, 0:128 * (e - j):d],
                   OP.is_lt, [("P", 256 * j, 256 * e), b], [("WN", 256 * j, 256 * e)], waw=False)

        def votes(c, b, first=0, end=16):
            for q in range(first, end):
                mm(T[b][:, 64 * c:64 * c + 64], T.EV[:, 15 - q:143 - q], T.WN[:, 4 * c:4 * c + 4, 16 * q:16 * q + 16],
                   q == 0, q == 15, ["EV", ("WN", CW * c, CW * c + CW)], [b])

        def prefix(j, e):
            scan(T.PM[:, OFF + 256 * j:OFF + 256 * e], T.RS[:, 0:256 * (e - j)], T.P[:, 256 * j:256 * e], OP.mult, OP.max,
                 ["RS", ("P", 256 * j, 256 * e)], [("PM", OFF + 256 * j, OFF + 256 * e)])

        def run(i, C, ini, j, e, b):
            back = slice(16 * e - 1, 16 * j - 1 if j else None, -1)
            scan(T.st[:, i, back], T[b][:, back], T[C][:, back], OP.min, OP.max, [b, C],
                 [("st", 256 * i + 16 * j, 256 * i + 16 * e)], ini=ini)

        def lists(j, e):
            ts(T.kl[:, :, j:e], T.st[:, :, 16 * j + 1:16 * e:16], -float(BASE), None, OP.add, None,
               [("st", 16 * j, 16 * e), ("st", 256 + 16 * j, 256 + 16 * e)], [("kl", j, e), ("kl", 16 + j, 16 + e)])

        def list_one(i, j, e):
            ts(T.kl[:, i, j:e], T.st[:, i, 16 * j + 1:16 * e:16], -float(BASE), None, OP.add, None,
               [("st", 256 * i + 16 * j, 256 * i + 16 * e)], [("kl", 16 * i + j, 16 * i + e)])

        def by_k(x, q, j, e):
            by_list(q, T[x + "F"][:, 16 * j:16 * e], T[x + "T"][:, 0:16].indirect(T.kl[:, 0, j:e]), [x + "T", ("kl", j, e)],
                    [(x + "F", 16 * j, 16 * e)])

        def values(j, e):
            tt(T.D[:, 16 * j:16 * e], T.PM[:, 0:OFF + 256 * e].indirect(T.kl[:, 1, j:e]), T.P[:, 256 * j:256 * e:16],
               OP.subtract, [("PM", 0, OFF + 256 * e), ("kl", 16 + j, 16 + e), ("P", 256 * j, 256 * e)], [("D", 16 * j, 16 * e)])

        def largest(j, e, b):
            act(T.D[:, 16 * j:16 * e], T.PM[:, 0:OFF + 256 * e].indirect(T.kl[:, 1, j:e]), AF.Copy,
                [("PM", 0, OFF + 256 * e), ("kl", 16 + j, 16 + e)], [("D", 16 * j, 16 * e)])
            mm(T[b][:, 16 * j:16 * e], T.NI[:], T.P[:, 256 * j:256 * e:16], True, False, ["NI", ("P", 256 * j, 256 * e)], [b])
            mm(T[b][:, 16 * j:16 * e], T.ID[:], T.D[:, 16 * j:16 * e], False, True, ["ID", ("D", 16 * j, 16 * e)], [b])

        def sizes(j, e, b="D"):
            act(T.Y2[:, 32 * j:32 * e:2], T[b][:, 16 * j:16 * e], AF.Abs, [(b, 16 * j, 16 * e)], [("Y2", 32 * j, 32 * e)])

        def listed():
            for q in range(16):
                mm(psL, T.WE[:, 15 - q:143 - q], T.Y2[:, 2 * q:512:32], False, q == 15, ["WE", "Y2"], ["psL"])

        def listed_o():
            for q in range(16):
                mm(psO, T.E0[:, 15 - q:143 - q], T.G[:, q:SLOTS:16], q == 0, q == 15, ["E0", "G"], ["psO"])

        def masks(j, e, b, stop=0):
            a, e, by = 16 * j, 16 * e, {"ps2": "MI", "ps3": "M3"}[b]
            mm(T[b][:, a:e], T[by][:], T.NF[:, a:e], False, bool(stop), [by, ("NF", a, e)], [b])

        def places(j, e, b, stop=0):
            mm(T[b][:, 16 * j:16 * e], T.WB[:], T.Y2[:, 32 * j:32 * e:2], False, bool(stop), ["WB", ("Y2", 32 * j, 32 * e)], [b])

        def sums(x, j, e):
            a, e, out, src = 16 * j, 16 * e, x + "C", x + "F"
            scan(T[out][:, a:e], T.ob[:, a:e], T[src][:, a:e], OP.mult, OP.add,
                 ["ob", (src, a, e)] + ([(out, a - 1, a)] if a else []), [(out, a, e)], ini=T[out][:, a - 1:a] if a else 0.0)

        def adds(b):
            out, by = {"ps2": (ps2, T.m16[:]), "ps3": (ps3, T.m4k[:]), "psL": (psL, T.m4k[:, 0:16])}[b]
            mm(out, T.BA[:], by, False, False, ["BA", "m16", "m4k"], [b])

        def count(j, e, acc):
            a, e, src = 16 * j, 16 * e, acc[0] + "C"
            for c in range(2):
                r = c + 2 * (src == "ZC")
                act(T.J[:, r, a:e], T[src][:, a:e], AF.Sign, [(src, a, e), "bs"], [("J", 256 * r + a, 256 * r + e), (acc, c, c + 1)],
                    bias=T.bs[:, c:c + 1], scale=-1.0, accum_out=T[acc][:, c:c + 1])

        def lanes(x):
            a, b, out = x + "a", x + "b", x + "L"
            for c in range(2):
                ts(T[out][:, c:c + 1], T[b][:, c:c + 1], T[a][:, c:c + 1], 256.0, OP.add, OP.add, [a, b], [(out, c, c + 1)])

        def dumps(out, src, by, f):
            for c in range(2):
                act(T[out][:, c:c + 1], T[src][:, c:c + 1], f, [src, by], [(out, c, c + 1)], scale=4096.0, bias=T[by][:, c:c + 1])

        def targets():
            for c in range(2):
                ts(T.OL[:, c:c + 1], T.psO[:, c:c + 1], 2048.0, T.nd[:, c:c + 1], OP.add, OP.max, ["psO", "nd"], [("OL", c, c + 1)])

        def pass_on():
            send(dst, T[PK][:], T[RX][:], [PK], "arr%d" % t)
            landed(frm, "arr%d" % t, reg(RX))

        def stacks():
            if last:
                ts(T.yof[:], UJ, 0.0625, None, OP.mult, None, ["UJ"], ["yof"])
                dma("s", "out_yo", T.yo[:], T.yof[:], ["yof"], [])

        def take():
            tt(spare.indirect(T.OL[:, 0:2]), T.fo[:], T[RX][:, 0:SLOTS], OP.add, ["OL", "fo", RX], [("B", 0, NB + SLOTS)])
            if last:
                dma("y", "out_yb", T.yb[:], balls, [("B", 0, NB)], [])

        steps = {
            "tops": tops, "compare": compare, "halves": halves,
            "Sh": lambda: ts(T.Sh[:], T.SU[:], -2048.0, None, OP.add, None, ["SU"], ["Sh"]) if t else None,
            "listedO": listed_o,
            "WB": lambda: None if t else ts(T.WB[:], T.BO[:], T.wf[:], None, OP.mult, None, ["BO", "wf"], ["WB"]),
            "gather": gather, "votes": votes, "prefix": prefix, "lists": lists,
            "list": list_one, "by_k": by_k, "values": values, "largest": largest, "sizes": sizes, "listed": listed,
            "masks": masks, "places": places, "sums": sums, "adds": adds, "count": count, "lanes": lanes, "OL": targets,
            "send": pass_on, "stacks": stacks, "take": take,
            "sooner": lambda a, e: None if last else offsets(a, e), "later": lambda a, e: offsets(a, e) if t else None,
            "begin3": lambda: mm(ps3, T.ob[0:3, 0:128], T.c3[0:3, :], True, False, ["ob", "c3"], ["ps3"]),
            "beginL": lambda: mm(psL, T.ID[:], T.iL[:], True, False, ["ID", "iL"], ["psL"]),
            "run0": lambda j, e, b: run(0, "C0", BASE + 15.0, j, e, b),
            "run1": lambda j, e, b: run(1, "C1", T.C1[:, 16 * e:16 * e + 1], j, e, b),
            "ksum": lambda: scan(T.ks[:], T.kc[:], T.st[:, 0, 1:256:16], OP.add, OP.add, ["kc", ("st", 0, 256)], ["ks"]),
            "kblocks": lambda: ts(T.BA[:], T.BO[:], T.ks[:, 15:16], -1.0, OP.mult, OP.mult, ["BO", "ks"], ["BA"]),
            "VI": lambda: cp(T.VI[:], psL, ["psL"], ["VI"]),
            "VB": lambda: ts(T.VB[:], T.VI[:], 4, 4095, OP.arith_shift_right, OP.bitwise_and, ["VI"], ["VB"]),
            "VL": lambda: cp(T.VL[:], T.VB[:], ["VB"], ["VL"]),
            "own": lambda: cp(spare.indirect(T.VL[:, 0:16]), T.Y2[:, 0:512:2], ["VL", "Y2"], [("B", 0, NB + SLOTS)]),
            "first": lambda: tt(T.m1[:], ps2, UJ, OP.max, ["ps2", "UJ"], ["m1"]),
            "second": lambda: tt(T.UI[:], ps3, T.m1[:], OP.max, ["ps3", "m1"], ["UI"]),
            "UJ": lambda: ts(UJ, T.UI[:], 0xFFF0, None, OP.bitwise_and, None, ["UI"], ["UJ"]),
            "G": lambda: ts(T.G[:], T.UJ[:, 0:528].indirect(T.ZL[:, 0:2]), 0.0625, -2048.0, OP.mult, OP.add, ["UJ", "ZL"], ["G"]),
            "dumps0": lambda: dumps("na", "Za", "nb", AF.Identity), "dumps1": lambda: dumps("nd", "Zb", "na", AF.Relu),
            "pack": lambda: act(T[PK][:, 0:SLOTS], T.Y2[:, 0:528].indirect(T.HL[:, 0:2]), AF.Copy, ["Y2", "HL"], [(PK, 0, SLOTS)]),
            "OW": lambda: act(T.OW[:], T.Y2[:, 0:528].indirect(T.ZL[:, 0:2]), AF.Copy, ["Y2", "ZL"], ["OW"]),
            "flags": lambda: ts(T[PK][:, SLOTS:64], T.QT[:], T.HC[:, 255:256], None, OP.is_ge, None, ["QT", ("HC", 255, 256)],
                                [(PK, SLOTS, 64)]),
            "keep": lambda: tt(T.fo[:], T[RX][:, SLOTS:64], T.OW[:], OP.mult, [RX, "OW"], ["fo"]),
        }
        steps.update(ahead)
        words = ORDER.split()
        if t == 0:
            words = [w for w in words if w.split(":")[0] != "factors"]
            cut = words.index("send") + 1
            words = ([w for w in words[:cut] if w not in AFTER] + [w for w in words[:cut] if w in AFTER] + words[cut:])
        for word in words:
            name, *args = word.split(":")
            steps[name](*[int(a) if a.isdigit() else a for a in args])

    for t in range(ROUNDS):
        throw(t)

    for sem in sorted(total, key=lambda s: s == "dma_out_yb"):
        wait_for("g", sem, total[sem], {})
